import numpy as np
import ml_dtypes


def mxq(x, axis, fmt="e4m3"):
    dtype, down = {"e4m3": (ml_dtypes.float8_e4m3fn, 7), "e5m2": (ml_dtypes.float8_e5m2, 14)}[fmt]
    v = np.moveaxis(np.asarray(x, np.float32).astype(ml_dtypes.bfloat16).astype(np.float64), axis, -1)
    blocks = v.reshape(v.shape[:-1] + (-1, 32))
    amax = np.abs(blocks).max(-1, keepdims=True)
    byte = np.maximum(np.where(amax > 0, np.frexp(amax)[1] - 1 + 127, 0) - down, 1)
    scale = np.exp2(byte - 127.0)
    codes = (blocks / scale).astype(np.float32).astype(dtype).astype(np.float64)
    return np.moveaxis((codes * scale).reshape(v.shape), -1, axis)


WIDE = False


def mx_kscale(k):
    if not WIDE:
        return np.ones(k)
    levels = np.array([10, -10, 5, -5, 0])
    if k % 512:
        return np.exp2(np.random.permutation(np.resize(levels, k // 32))).repeat(32)
    a = np.empty((k // 512, 16))
    for p in range(k // 512):
        a[p, :8] = np.random.permutation(np.resize(levels, 8))
        for g in range(8):
            far = levels[np.abs(levels - a[p, g]) >= 10]
            a[p, g + 8] = far[np.random.randint(len(far))]
    return np.exp2(a.ravel()).repeat(32)


def f64(x):
    return np.asarray(x).astype(np.float64)


def striped(idx):
    return np.tile(np.asarray(idx).reshape(-1, 16).T, (8, 1)).astype(np.uint16)


def unstriped(offs):
    return offs[:16].T.reshape(-1).astype(np.int64)


E2M1 = np.array([0.0, 0.5, 1.0, 1.5, 2.0, 3.0, 4.0, 6.0, -0.0, -0.5, -1.0, -1.5, -2.0, -3.0, -4.0, -6.0])


def pack_weight(w, fmt):
    k, n = w.shape
    w = f64(np.asarray(w, np.float32).astype(ml_dtypes.bfloat16)).reshape(k // 32, 32, n)
    amax = np.abs(w).max(1)
    if fmt == "e4m3":
        byte = np.frexp(amax)[1] - 1 + 127 - 7
    else:
        mant, ex = np.frexp(amax / 6.0)
        byte = np.where(mant > 0.5, ex, ex - 1) + 127
    byte = np.clip(np.where(amax > 0, byte, 1), 1, 254)
    scaled = (w * np.exp2(127.0 - byte)[:, None, :]).reshape(k, n).astype(np.float32)
    by_word = np.ascontiguousarray(scaled.reshape(k // 512, 128, 4, n).transpose(0, 1, 3, 2))
    if fmt == "e4m3":
        words = by_word.astype(ml_dtypes.float8_e4m3fn).view(np.uint8)
    else:
        c = by_word.astype(ml_dtypes.float4_e2m1fn).view(np.uint8) & 0xF
        words = (c[..., 0::2] | (c[..., 1::2] << 4)).reshape(k // 512, 128, 2 * n)
    return np.ascontiguousarray(words), np.ascontiguousarray(byte.astype(np.uint8).reshape(k // 512, 16, n))


def unpack_weight(words, scales, fmt):
    g, _, n = scales.shape
    words = np.ascontiguousarray(words).reshape(g, 128, n, -1)
    if fmt == "e4m3":
        vals = words.view(ml_dtypes.float8_e4m3fn).astype(np.float64)
    else:
        nib = np.empty((g, 128, n, 4), np.uint8)
        nib[..., 0::2] = words & 0xF
        nib[..., 1::2] = words >> 4
        vals = E2M1[nib]
    vals = vals * np.repeat(np.exp2(scales.astype(np.float64) - 127.0), 8, axis=1)[..., None]
    return vals.transpose(0, 1, 3, 2).reshape(g * 512, n)


def sigmoid(v):
    return 1.0 / (1.0 + np.exp(-v))


B, N, T, D, NQ = 1, 512, 2048, 1024, 512
SEG = 32


def setup_inputs():
    n = np.random.standard_normal
    idx = np.random.permutation(T)[:B * N]
    s = mx_kscale(D)[:, None]
    kp = pack_weight(n((D, T)) / s, "e2m1")
    return {
        "qT": (n((B, D, NQ)) * s * (1.00 / np.sqrt(D))).astype(np.float32),
        "k_words": np.ascontiguousarray(kp[0].reshape(1, 2, 128, T, 2).transpose(0, 2, 3, 1, 4)).reshape(1, 128, T, 4),
        "k_scales": kp[1],
        "tt": np.tile(n(2048) + 1, (128, 1)).astype(np.float32),
        "offs": striped(idx),
    }


def reference(qT, k_words, k_scales, tt, offs):
    idx = unstriped(offs)
    pick = lambda x, which: x[:, which].reshape(x.shape[0], B, -1).transpose(1, 0, 2)
    k = unpack_weight(k_words.reshape(1, 128, T, 2, 2).transpose(0, 3, 1, 2, 4).reshape(2, 128, 2 * T), k_scales, "e2m1")
    kg = pick(k, idx)
    qq = mxq(f64(qT), 1, "e4m3")
    a = kg.transpose(0, 2, 1) @ qq
    y = sigmoid(4.0 * (a - pick(f64(tt), idx)[:, :1, :].transpose(0, 2, 1))).reshape(B, N, NQ // SEG, SEG).sum(-1)
    return y

@@ -1,0 +1,170 @@
+from contextlib import ExitStack
+
+import concourse.mybir as mybir
+from concourse.masks import make_identity
+
+P = 128
+PACK = 4
+K_PASS = P * PACK
+D, T, SLOTS, NQ, SEG = 1024, 2048, 512, 512, 32
+PASSES = D // K_PASS
+BLOCKS = SLOTS // P
+HALF = 256
+HALVES = NQ // HALF
+N_MM = 128
+SHARP = 4.0
+LIVE = 96
+
+F32 = mybir.dt.float32
+BF16 = mybir.dt.bfloat16
+I32 = mybir.dt.int32
+U32 = mybir.dt.uint32
+U16 = mybir.dt.uint16
+U8 = mybir.dt.uint8
+FP8X4 = mybir.dt.float8_e4m3fn_x4
+FP4X4 = mybir.dt.float4_e2m1fn_x4
+ACT = mybir.ActivationFunctionType
+
+FLOPS = 2 * SLOTS * NQ * D
+BYTES = 4 * D * NQ + P * T * 4 + PASSES * 16 * T + 4 * T + 2 * P * SLOTS // 16 + 4 * SLOTS * NQ // SEG
+
+
+def tile_attend_tok_votets_topk_kernel(tc, qT, k_words, k_scales, tt, offs, out):
+    nc = tc.nc
+    with ExitStack() as ctx:
+        held = ctx.enter_context(tc.tile_pool(name="held", bufs=1))
+        psum = ctx.enter_context(tc.psum_pool(name="psum", bufs=8))
+
+        offsets = held.tile([P, SLOTS // 16], U16, name="offsets")
+        nc.sync.dma_start(offsets[:], offs)
+
+        scale_pool = held.tile([P, T], U8, name="scale_pool", tag="early_late", align_bytes=64)
+        nc.sync.dma_start(
+            scale_pool[LIVE:P, :].bitcast(I32), k_scales.rearrange("o f t -> f o t").bitcast(I32)
+        )
+        nc.vector.memset(scale_pool[0:LIVE, :].bitcast(I32), 0)
+        tt_pool = held.tile([P, T], F32, name="tt_pool")
+        nc.vector.memset(tt_pool[:], 0.0)
+
+        ident = held.tile([P, P], F32, name="ident")
+        make_identity(nc, ident[:])
+        warm_out = held.tile([P, 8], F32, name="warm_out")
+        nc.scalar.activation(warm_out[:], ident[:, 0:8], ACT.Sigmoid)
+        key_scales = held.tile([P, PASSES, SLOTS], U8, name="key_scales", align_bytes=64)
+        nc.gpsimd.memset(key_scales[:].rearrange("p o n -> p (o n)").bitcast(I32), 0)
+
+        word_pool = held.tile([P, T], U32, name="word_pool", align_bytes=64)
+        nc.sync.dma_start(
+            word_pool[:].bitcast(I32), k_words[0].rearrange("p t b -> p (t b)").bitcast(I32)
+        )
+
+        chunks = [(h, o) for h in range(HALVES) for o in range(PASSES)]
+
+        def load_chunk(dst, h, o):
+            rows = qT[0, o * K_PASS : (o + 1) * K_PASS, h * HALF : (h + 1) * HALF]
+            nc.sync.dma_start(dst, rows.rearrange("(p j) w -> p j w", j=PACK))
+
+        raw_first = held.tile([P, PACK, HALF], F32, name="raw_first")
+        raw = {chunks[0]: raw_first[:]}
+        load_chunk(raw_first[:], *chunks[0])
+        nc.sync.dma_start(tt_pool[0:1, :], tt[0:1, :])
+
+        picked_scales = held.tile([P, SLOTS], U8, name="picked_scales", align_bytes=64)
+        nc.vector.tensor_copy(picked_scales[:], scale_pool[:].indirect(offsets[:]))
+        raw_rest = held.tile([P, len(chunks) - 1, PACK, HALF], F32, name="raw_rest", tag="early_late", align_bytes=64)
+        for i, chunk in enumerate(chunks[1:]):
+            raw[chunk] = raw_rest[:, i]
+        load_chunk(raw[chunks[1]], *chunks[1])
+        for quad in range(4):
+            nc.sync.dma_start(
+                key_scales[32 * quad : 32 * quad + 4].rearrange("p o n -> p (o n)").bitcast(I32),
+                picked_scales[LIVE + 8 * quad : LIVE + 8 * quad + 8, :].bitcast(I32),
+            )
+        for chunk in chunks[2:]:
+            load_chunk(raw[chunk], *chunk)
+
+        picked_words = held.tile([P, SLOTS], U32, name="picked_words", align_bytes=64)
+        nc.vector.tensor_copy(picked_words[:], word_pool[:].indirect(offsets[:]))
+        key_words = held.tile([P, PASSES, SLOTS], U16, name="key_words", align_bytes=64)
+        nc.vector.tensor_copy(
+            key_words[:], picked_words[:].bitcast(U16).rearrange("p (n o) -> p o n", o=PASSES)
+        )
+
+        picked_tt = held.tile([P, SLOTS], F32, name="picked_tt")
+        nc.vector.tensor_copy(picked_tt[:], tt_pool[:].indirect(offsets[:]))
+        turned = psum.tile([P, BLOCKS, P], F32, name="turned", tag="bank")
+        for c in range(BLOCKS):
+            nc.tensor.transpose(turned[:, c, :], picked_tt[:, c * P : (c + 1) * P], ident[:])
+        bias = held.tile([P, BLOCKS], F32, name="bias")
+        nc.scalar.activation(bias[:], turned[:, :, 0], ACT.Copy, scale=-SHARP)
+
+        q_codes = held.tile([P, PASSES, NQ], U32, name="q_codes", align_bytes=64)
+        q_scales = held.tile([P, PASSES, NQ], U8, name="q_scales", align_bytes=64)
+        votes = held.tile([P, BLOCKS, NQ // SEG], F32, name="votes")
+
+        soft = held.tile([P, BLOCKS, NQ], F32, name="soft")
+        groups = [(c, n0) for c in range(BLOCKS) for n0 in range(0, HALF, N_MM)]
+
+        def quantise(h, o, copy):
+            grouped = held.tile([P, HALF, PACK], BF16, name="grouped%d%d" % (h, o), align_bytes=64)
+            copy(
+                grouped[:].rearrange("p (c i) t -> p c t i", i=4),
+                raw[h, o].rearrange("p t (c i) -> p c t i", i=4),
+            )
+            cols = slice(h * HALF, (h + 1) * HALF)
+            nc.vector.quantize_mx(
+                out=q_codes[:, o, cols].bitcast(FP8X4),
+                scales=q_scales[:, o, cols],
+                in_=grouped[:].rearrange("p w t -> p (w t)"),
+            )
+
+        def multiply(acc, h, o, c, n0):
+            slots = slice(c * P, (c + 1) * P)
+            cols = slice(h * HALF + n0, h * HALF + n0 + N_MM)
+            nc.tensor.matmul_mx(
+                out=acc[:],
+                lhsT=key_words[:, o, slots].bitcast(FP4X4),
+                lhsT_scale=key_scales[:, o, slots],
+                rhs=q_codes[:, o, cols].bitcast(FP8X4),
+                rhs_scale=q_scales[:, o, cols],
+                start=(o == 0),
+                stop=(o == PASSES - 1),
+            )
+
+        def open_groups(h):
+            accs = {}
+            for c, n0 in groups:
+                accs[c, n0] = psum.tile([P, N_MM], F32, name="acc", tag="bank")
+                multiply(accs[c, n0], h, 0, c, n0)
+            return accs
+
+        def close_groups(accs, h):
+            for c, n0 in groups:
+                multiply(accs[c, n0], h, 1, c, n0)
+                cols = slice(h * HALF + n0, h * HALF + n0 + N_MM)
+                nc.scalar.activation(
+                    soft[:, c, cols], accs[c, n0][:], ACT.Sigmoid, bias=bias[:, c : c + 1], scale=SHARP
+                )
+
+        def count(h, c):
+            runs = slice(h * HALF // SEG, (h + 1) * HALF // SEG)
+            nc.vector.tensor_reduce(
+                votes[:, c, runs],
+                soft[:, c, h * HALF : (h + 1) * HALF].rearrange("p (j r) -> p j r", r=SEG),
+                mybir.AxisListType.X,
+                mybir.AluOpType.add,
+            )
+
+        quantise(0, 0, nc.scalar.copy)
+        accs = open_groups(0)
+        quantise(0, 1, nc.scalar.copy)
+        quantise(1, 0, nc.vector.tensor_copy)
+        close_groups(accs, 0)
+        quantise(1, 1, nc.vector.tensor_copy)
+        accs = open_groups(1)
+        for c in range(BLOCKS):
+            count(0, c)
+        close_groups(accs, 1)
+        for c in range(BLOCKS):
+            count(1, c)
+            nc.sync.dma_start(out[0, c * P : (c + 1) * P, :], votes[:, c, :])

@@ -38,18 +38,21 @@ def tile_attend_tok_votets_topk_kernel(tc, qT, k_words, k_scales, tt, offs, out)
         offsets = held.tile([P, SLOTS // 16], U16, name="offsets")
         nc.sync.dma_start(offsets[:], offs)
 
-        scale_pool = held.tile([P, T], U8, name="scale_pool", tag="early_late", align_bytes=64)
-        nc.sync.dma_start(
+        scale_pool = held.tile([P, T], U8, name="scale_pool", align_bytes=64)
+        nc.scalar.dma_start(
             scale_pool[LIVE:P, :].bitcast(I32), k_scales.rearrange("o f t -> f o t").bitcast(I32)
         )
-        nc.vector.memset(scale_pool[0:LIVE, :].bitcast(I32), 0)
-        tt_pool = held.tile([P, T], F32, name="tt_pool")
+        tt_pool = held.tile([P, T], F32, name="tt_pool", tag="tt_then_words", align_bytes=64)
         nc.vector.memset(tt_pool[:], 0.0)
+        nc.scalar.dma_start(tt_pool[0:1, :], tt[0:1, :])
+        nc.vector.memset(scale_pool[0:LIVE, :].bitcast(I32), 0)
+        warm = held.tile([P, 8], F32, name="warm")
+        nc.vector.memset(warm[:], 0.0)
+        warm_out = held.tile([P, 8], F32, name="warm_out")
+        nc.scalar.activation(warm_out[:], warm[:], ACT.Sigmoid)
 
         ident = held.tile([P, P], F32, name="ident")
         make_identity(nc, ident[:])
-        warm_out = held.tile([P, 8], F32, name="warm_out")
-        nc.scalar.activation(warm_out[:], ident[:, 0:8], ACT.Sigmoid)
         key_scales = held.tile([P, PASSES, SLOTS], U8, name="key_scales", align_bytes=64)
         nc.gpsimd.memset(key_scales[:].rearrange("p o n -> p (o n)").bitcast(I32), 0)
 
@@ -58,64 +61,63 @@ def tile_attend_tok_votets_topk_kernel(tc, qT, k_words, k_scales, tt, offs, out)
             word_pool[:].bitcast(I32), k_words[0].rearrange("p t b -> p (t b)").bitcast(I32)
         )
 
-        chunks = [(h, o) for h in range(HALVES) for o in range(PASSES)]
+        raw = {}
 
-        def load_chunk(dst, h, o):
+        def load_chunk(h, o):
+            raw[h, o] = held.tile([P, PACK, HALF], F32, name="raw%d%d" % (h, o))
             rows = qT[0, o * K_PASS : (o + 1) * K_PASS, h * HALF : (h + 1) * HALF]
-            nc.sync.dma_start(dst, rows.rearrange("(p j) w -> p j w", j=PACK))
+            nc.sync.dma_start(raw[h, o][:], rows.rearrange("(p j) w -> p j w", j=PACK))
 
-        raw_first = held.tile([P, PACK, HALF], F32, name="raw_first")
-        raw = {chunks[0]: raw_first[:]}
-        load_chunk(raw_first[:], *chunks[0])
-        nc.sync.dma_start(tt_pool[0:1, :], tt[0:1, :])
+        load_chunk(0, 0)
+        load_chunk(0, 1)
 
         picked_scales = held.tile([P, SLOTS], U8, name="picked_scales", align_bytes=64)
         nc.vector.tensor_copy(picked_scales[:], scale_pool[:].indirect(offsets[:]))
-        raw_rest = held.tile([P, len(chunks) - 1, PACK, HALF], F32, name="raw_rest", tag="early_late", align_bytes=64)
-        for i, chunk in enumerate(chunks[1:]):
-            raw[chunk] = raw_rest[:, i]
-        load_chunk(raw[chunks[1]], *chunks[1])
         for quad in range(4):
             nc.sync.dma_start(
                 key_scales[32 * quad : 32 * quad + 4].rearrange("p o n -> p (o n)").bitcast(I32),
                 picked_scales[LIVE + 8 * quad : LIVE + 8 * quad + 8, :].bitcast(I32),
             )
-        for chunk in chunks[2:]:
-            load_chunk(raw[chunk], *chunk)
+        load_chunk(1, 0)
+        load_chunk(1, 1)
 
-        picked_words = held.tile([P, SLOTS], U32, name="picked_words", align_bytes=64)
+        picked_tt = held.tile([P, SLOTS], F32, name="picked_tt")
+        nc.vector.tensor_copy(picked_tt[:], tt_pool[:].indirect(offsets[:]))
+
+        picked_words = held.tile([P, SLOTS], U32, name="picked_words", tag="tt_then_words", align_bytes=64)
         nc.vector.tensor_copy(picked_words[:], word_pool[:].indirect(offsets[:]))
         key_words = held.tile([P, PASSES, SLOTS], U16, name="key_words", align_bytes=64)
         nc.vector.tensor_copy(
             key_words[:], picked_words[:].bitcast(U16).rearrange("p (n o) -> p o n", o=PASSES)
         )
 
-        picked_tt = held.tile([P, SLOTS], F32, name="picked_tt")
-        nc.vector.tensor_copy(picked_tt[:], tt_pool[:].indirect(offsets[:]))
         turned = psum.tile([P, BLOCKS, P], F32, name="turned", tag="bank")
         for c in range(BLOCKS):
             nc.tensor.transpose(turned[:, c, :], picked_tt[:, c * P : (c + 1) * P], ident[:])
         bias = held.tile([P, BLOCKS], F32, name="bias")
         nc.scalar.activation(bias[:], turned[:, :, 0], ACT.Copy, scale=-SHARP)
 
-        q_codes = held.tile([P, PASSES, NQ], U32, name="q_codes", align_bytes=64)
+        q_codes = held.tile([P, PASSES, NQ], U32, name="q_codes", tag="tt_then_words", align_bytes=64)
         q_scales = held.tile([P, PASSES, NQ], U8, name="q_scales", align_bytes=64)
-        votes = held.tile([P, BLOCKS, NQ // SEG], F32, name="votes")
 
         soft = held.tile([P, BLOCKS, NQ], F32, name="soft")
         groups = [(c, n0) for c in range(BLOCKS) for n0 in range(0, HALF, N_MM)]
 
-        def quantise(h, o, copy):
-            grouped = held.tile([P, HALF, PACK], BF16, name="grouped%d%d" % (h, o), align_bytes=64)
+        grouped = {}
+
+        def interleave(copy, h, o, n0, tag):
+            grouped[h, o, n0] = held.tile([P, N_MM, PACK], BF16, name="grouped", tag=tag, align_bytes=64)
             copy(
-                grouped[:].rearrange("p (c i) t -> p c t i", i=4),
-                raw[h, o].rearrange("p t (c i) -> p c t i", i=4),
+                grouped[h, o, n0][:].rearrange("p (c i) t -> p c t i", i=4),
+                raw[h, o][:, :, n0 : n0 + N_MM].rearrange("p t (c i) -> p c t i", i=4),
             )
-            cols = slice(h * HALF, (h + 1) * HALF)
+
+        def quantise(h, o, n0):
+            cols = slice(h * HALF + n0, h * HALF + n0 + N_MM)
             nc.vector.quantize_mx(
                 out=q_codes[:, o, cols].bitcast(FP8X4),
                 scales=q_scales[:, o, cols],
-                in_=grouped[:].rearrange("p w t -> p (w t)"),
+                in_=grouped[h, o, n0][:].rearrange("p w t -> p (w t)"),
             )
 
         def multiply(acc, h, o, c, n0):
@@ -138,33 +140,47 @@ def tile_attend_tok_votets_topk_kernel(tc, qT, k_words, k_scales, tt, offs, out)
                 multiply(accs[c, n0], h, 0, c, n0)
             return accs
 
-        def close_groups(accs, h):
-            for c, n0 in groups:
+        def close_groups(accs, h, order):
+            for c, n0 in order:
                 multiply(accs[c, n0], h, 1, c, n0)
                 cols = slice(h * HALF + n0, h * HALF + n0 + N_MM)
                 nc.scalar.activation(
                     soft[:, c, cols], accs[c, n0][:], ACT.Sigmoid, bias=bias[:, c : c + 1], scale=SHARP
                 )
 
-        def count(h, c):
-            runs = slice(h * HALF // SEG, (h + 1) * HALF // SEG)
+        def count(c0, c1, q0, q1):
             nc.vector.tensor_reduce(
-                votes[:, c, runs],
-                soft[:, c, h * HALF : (h + 1) * HALF].rearrange("p (j r) -> p j r", r=SEG),
+                votes[:, c0:c1, q0 // SEG : q1 // SEG],
+                soft[:, c0:c1, q0:q1].rearrange("p c (j r) -> p c j r", r=SEG),
                 mybir.AxisListType.X,
                 mybir.AluOpType.add,
             )
 
-        quantise(0, 0, nc.scalar.copy)
+        on_scalar, on_vector = nc.scalar.copy, nc.vector.tensor_copy
+        interleave(on_scalar, 0, 0, 0, "g0")
+        interleave(on_scalar, 0, 0, N_MM, "g1")
+        quantise(0, 0, 0)
+        quantise(0, 0, N_MM)
         accs = open_groups(0)
-        quantise(0, 1, nc.scalar.copy)
-        quantise(1, 0, nc.vector.tensor_copy)
-        close_groups(accs, 0)
-        quantise(1, 1, nc.vector.tensor_copy)
+        interleave(on_scalar, 0, 1, 0, "g2")
+        interleave(on_vector, 0, 1, N_MM, "g0")
+        quantise(0, 1, 0)
+        quantise(0, 1, N_MM)
+        close_groups(accs, 0, groups)
+        interleave(on_vector, 1, 0, 0, "g3")
+        interleave(on_vector, 1, 0, N_MM, "g4")
+        quantise(1, 0, 0)
+        quantise(1, 0, N_MM)
         accs = open_groups(1)
+        interleave(on_vector, 1, 1, 0, "g5")
+        interleave(on_scalar, 1, 1, N_MM, "g6")
+        quantise(1, 1, 0)
+        quantise(1, 1, N_MM)
+        votes = held.tile([P, BLOCKS, NQ // SEG], F32, name="votes", tag="g4", align_bytes=64)
         for c in range(BLOCKS):
-            count(0, c)
-        close_groups(accs, 1)
+            count(c, c + 1, 0, HALF)
+        close_groups(accs, 1, [(c, n0) for n0 in range(0, HALF, N_MM) for c in range(BLOCKS)])
+        count(0, BLOCKS, HALF, HALF + N_MM)
         for c in range(BLOCKS):
-            count(1, c)
+            count(c, c + 1, HALF + N_MM, NQ)
             nc.sync.dma_start(out[0, c * P : (c + 1) * P, :], votes[:, c, :])

@@ -14,6 +14,7 @@ HALVES = NQ // HALF
 N_MM = 128
 SHARP = 4.0
 LIVE = 96
+PIECE = 256
 
 F32 = mybir.dt.float32
 BF16 = mybir.dt.bfloat16
@@ -39,27 +40,19 @@ def tile_attend_tok_votets_topk_kernel(tc, qT, k_words, k_scales, tt, offs, out)
         nc.sync.dma_start(offsets[:], offs)
 
         scale_pool = held.tile([P, T], U8, name="scale_pool", align_bytes=64)
-        nc.scalar.dma_start(
+        nc.sync.dma_start(
             scale_pool[LIVE:P, :].bitcast(I32), k_scales.rearrange("o f t -> f o t").bitcast(I32)
         )
-        tt_pool = held.tile([P, T], F32, name="tt_pool", tag="tt_then_words", align_bytes=64)
-        nc.vector.memset(tt_pool[:], 0.0)
-        nc.scalar.dma_start(tt_pool[0:1, :], tt[0:1, :])
+        tt_pool = held.tile([P, T], F32, name="tt_pool", tag="tt_then_codes", align_bytes=64)
+        nc.vector.memset(tt_pool[:].bitcast(I32), 0)
         nc.vector.memset(scale_pool[0:LIVE, :].bitcast(I32), 0)
-        warm = held.tile([P, 8], F32, name="warm")
-        nc.vector.memset(warm[:], 0.0)
-        warm_out = held.tile([P, 8], F32, name="warm_out")
-        nc.scalar.activation(warm_out[:], warm[:], ACT.Sigmoid)
 
         ident = held.tile([P, P], F32, name="ident")
         make_identity(nc, ident[:])
+        warm_out = held.tile([P, 8], F32, name="warm_out")
+        nc.scalar.activation(warm_out[:], ident[:, 0:8], ACT.Sigmoid)
         key_scales = held.tile([P, PASSES, SLOTS], U8, name="key_scales", align_bytes=64)
         nc.gpsimd.memset(key_scales[:].rearrange("p o n -> p (o n)").bitcast(I32), 0)
-
-        word_pool = held.tile([P, T], U32, name="word_pool", align_bytes=64)
-        nc.sync.dma_start(
-            word_pool[:].bitcast(I32), k_words[0].rearrange("p t b -> p (t b)").bitcast(I32)
-        )
 
         raw = {}
 
@@ -69,6 +62,11 @@ def tile_attend_tok_votets_topk_kernel(tc, qT, k_words, k_scales, tt, offs, out)
             nc.sync.dma_start(raw[h, o][:], rows.rearrange("(p j) w -> p j w", j=PACK))
 
         load_chunk(0, 0)
+        nc.sync.dma_start(tt_pool[0:1, :], tt[0:1, :])
+        word_pool = held.tile([P, T], U32, name="word_pool", align_bytes=64)
+        nc.sync.dma_start(
+            word_pool[:].bitcast(I32), k_words[0].rearrange("p t b -> p (t b)").bitcast(I32)
+        )
         load_chunk(0, 1)
 
         picked_scales = held.tile([P, SLOTS], U8, name="picked_scales", align_bytes=64)
@@ -84,12 +82,14 @@ def tile_attend_tok_votets_topk_kernel(tc, qT, k_words, k_scales, tt, offs, out)
         picked_tt = held.tile([P, SLOTS], F32, name="picked_tt")
         nc.vector.tensor_copy(picked_tt[:], tt_pool[:].indirect(offsets[:]))
 
-        picked_words = held.tile([P, SLOTS], U32, name="picked_words", tag="tt_then_words", align_bytes=64)
-        nc.vector.tensor_copy(picked_words[:], word_pool[:].indirect(offsets[:]))
+        picked_words = held.tile([P, SLOTS], U32, name="picked_words", align_bytes=64)
         key_words = held.tile([P, PASSES, SLOTS], U16, name="key_words", align_bytes=64)
-        nc.vector.tensor_copy(
-            key_words[:], picked_words[:].bitcast(U16).rearrange("p (n o) -> p o n", o=PASSES)
-        )
+        for s0 in range(0, SLOTS, PIECE):
+            piece = picked_words[:, s0 : s0 + PIECE]
+            nc.vector.tensor_copy(piece, word_pool[:].indirect(offsets[:, s0 // 16 : (s0 + PIECE) // 16]))
+            nc.vector.tensor_copy(
+                key_words[:, :, s0 : s0 + PIECE], piece.bitcast(U16).rearrange("p (n o) -> p o n", o=PASSES)
+            )
 
         turned = psum.tile([P, BLOCKS, P], F32, name="turned", tag="bank")
         for c in range(BLOCKS):
@@ -97,7 +97,7 @@ def tile_attend_tok_votets_topk_kernel(tc, qT, k_words, k_scales, tt, offs, out)
         bias = held.tile([P, BLOCKS], F32, name="bias")
         nc.scalar.activation(bias[:], turned[:, :, 0], ACT.Copy, scale=-SHARP)
 
-        q_codes = held.tile([P, PASSES, NQ], U32, name="q_codes", tag="tt_then_words", align_bytes=64)
+        q_codes = held.tile([P, PASSES, NQ], U32, name="q_codes", tag="tt_then_codes", align_bytes=64)
         q_scales = held.tile([P, PASSES, NQ], U8, name="q_scales", align_bytes=64)
 
         soft = held.tile([P, BLOCKS, NQ], F32, name="soft")
@@ -133,9 +133,9 @@ def tile_attend_tok_votets_topk_kernel(tc, qT, k_words, k_scales, tt, offs, out)
                 stop=(o == PASSES - 1),
             )
 
-        def open_groups(h):
+        def open_groups(h, order):
             accs = {}
-            for c, n0 in groups:
+            for c, n0 in order:
                 accs[c, n0] = psum.tile([P, N_MM], F32, name="acc", tag="bank")
                 multiply(accs[c, n0], h, 0, c, n0)
             return accs
@@ -161,9 +161,9 @@ def tile_attend_tok_votets_topk_kernel(tc, qT, k_words, k_scales, tt, offs, out)
         interleave(on_scalar, 0, 0, N_MM, "g1")
         quantise(0, 0, 0)
         quantise(0, 0, N_MM)
-        accs = open_groups(0)
+        accs = open_groups(0, groups)
         interleave(on_scalar, 0, 1, 0, "g2")
-        interleave(on_vector, 0, 1, N_MM, "g0")
+        interleave(on_vector, 0, 1, N_MM, "g7")
         quantise(0, 1, 0)
         quantise(0, 1, N_MM)
         close_groups(accs, 0, groups)
@@ -171,7 +171,8 @@ def tile_attend_tok_votets_topk_kernel(tc, qT, k_words, k_scales, tt, offs, out)
         interleave(on_vector, 1, 0, N_MM, "g4")
         quantise(1, 0, 0)
         quantise(1, 0, N_MM)
-        accs = open_groups(1)
+        by_columns = [(c, n0) for n0 in range(0, HALF, N_MM) for c in range(BLOCKS)]
+        accs = open_groups(1, by_columns)
         interleave(on_vector, 1, 1, 0, "g5")
         interleave(on_scalar, 1, 1, N_MM, "g6")
         quantise(1, 1, 0)
@@ -179,7 +180,7 @@ def tile_attend_tok_votets_topk_kernel(tc, qT, k_words, k_scales, tt, offs, out)
         votes = held.tile([P, BLOCKS, NQ // SEG], F32, name="votes", tag="g4", align_bytes=64)
         for c in range(BLOCKS):
             count(c, c + 1, 0, HALF)
-        close_groups(accs, 1, [(c, n0) for n0 in range(0, HALF, N_MM) for c in range(BLOCKS)])
+        close_groups(accs, 1, by_columns)
         count(0, BLOCKS, HALF, HALF + N_MM)
         for c in range(BLOCKS):
             count(c, c + 1, HALF + N_MM, NQ)

@@ -15,6 +15,7 @@ N_MM = 128
 SHARP = 4.0
 LIVE = 96
 PIECE = 256
+FUSED = 2
 
 F32 = mybir.dt.float32
 BF16 = mybir.dt.bfloat16
@@ -57,7 +58,7 @@ def tile_attend_tok_votets_topk_kernel(tc, qT, k_words, k_scales, tt, offs, out)
         raw = {}
 
         def load_chunk(h, o):
-            raw[h, o] = held.tile([P, PACK, HALF], F32, name="raw%d%d" % (h, o))
+            raw[h, o] = held.tile([P, PACK, HALF], F32, name="raw", tag="raw%d%d" % (h, o))
             rows = qT[0, o * K_PASS : (o + 1) * K_PASS, h * HALF : (h + 1) * HALF]
             nc.sync.dma_start(raw[h, o][:], rows.rearrange("(p j) w -> p j w", j=PACK))
 
@@ -100,7 +101,6 @@ def tile_attend_tok_votets_topk_kernel(tc, qT, k_words, k_scales, tt, offs, out)
         q_codes = held.tile([P, PASSES, NQ], U32, name="q_codes", tag="tt_then_codes", align_bytes=64)
         q_scales = held.tile([P, PASSES, NQ], U8, name="q_scales", align_bytes=64)
 
-        soft = held.tile([P, BLOCKS, NQ], F32, name="soft")
         groups = [(c, n0) for c in range(BLOCKS) for n0 in range(0, HALF, N_MM)]
 
         grouped = {}
@@ -112,10 +112,13 @@ def tile_attend_tok_votets_topk_kernel(tc, qT, k_words, k_scales, tt, offs, out)
                 raw[h, o][:, :, n0 : n0 + N_MM].rearrange("p t (c i) -> p c t i", i=4),
             )
 
-        def quantise(h, o, n0):
+        codes = {}
+
+        def quantise(h, o, n0, own_tile=None):
             cols = slice(h * HALF + n0, h * HALF + n0 + N_MM)
+            codes[h, o, n0] = q_codes[:, o, cols] if own_tile is None else own_tile[:]
             nc.vector.quantize_mx(
-                out=q_codes[:, o, cols].bitcast(FP8X4),
+                out=codes[h, o, n0].bitcast(FP8X4),
                 scales=q_scales[:, o, cols],
                 in_=grouped[h, o, n0][:].rearrange("p w t -> p (w t)"),
             )
@@ -127,7 +130,7 @@ def tile_attend_tok_votets_topk_kernel(tc, qT, k_words, k_scales, tt, offs, out)
                 out=acc[:],
                 lhsT=key_words[:, o, slots].bitcast(FP4X4),
                 lhsT_scale=key_scales[:, o, slots],
-                rhs=q_codes[:, o, cols].bitcast(FP8X4),
+                rhs=codes[h, o, n0].bitcast(FP8X4),
                 rhs_scale=q_scales[:, o, cols],
                 start=(o == 0),
                 stop=(o == PASSES - 1),
@@ -143,10 +146,26 @@ def tile_attend_tok_votets_topk_kernel(tc, qT, k_words, k_scales, tt, offs, out)
         def close_groups(accs, h, order):
             for c, n0 in order:
                 multiply(accs[c, n0], h, 1, c, n0)
-                cols = slice(h * HALF + n0, h * HALF + n0 + N_MM)
-                nc.scalar.activation(
-                    soft[:, c, cols], accs[c, n0][:], ACT.Sigmoid, bias=bias[:, c : c + 1], scale=SHARP
-                )
+                q0 = h * HALF + n0
+                if q0 + N_MM == NQ and c >= BLOCKS - FUSED:
+                    for r0 in range(0, N_MM, SEG):
+                        run = (q0 + r0) // SEG
+                        nc.scalar.activation(
+                            soft[:, c, q0 + r0 : q0 + r0 + SEG],
+                            accs[c, n0][:, r0 : r0 + SEG],
+                            ACT.Sigmoid,
+                            bias=bias[:, c : c + 1],
+                            scale=SHARP,
+                            accum_out=votes[:, c, run : run + 1],
+                        )
+                else:
+                    nc.scalar.activation(
+                        soft[:, c, q0 : q0 + N_MM],
+                        accs[c, n0][:],
+                        ACT.Sigmoid,
+                        bias=bias[:, c : c + 1],
+                        scale=SHARP,
+                    )
 
         def count(c0, c1, q0, q1):
             nc.vector.tensor_reduce(
@@ -163,25 +182,31 @@ def tile_attend_tok_votets_topk_kernel(tc, qT, k_words, k_scales, tt, offs, out)
         quantise(0, 0, N_MM)
         accs = open_groups(0, groups)
         interleave(on_scalar, 0, 1, 0, "g2")
-        interleave(on_vector, 0, 1, N_MM, "g7")
+        interleave(on_scalar, 0, 1, N_MM, "g7")
         quantise(0, 1, 0)
         quantise(0, 1, N_MM)
-        close_groups(accs, 0, groups)
-        interleave(on_vector, 1, 0, 0, "g3")
+        interleave(on_scalar, 1, 0, 0, "g3")
         interleave(on_vector, 1, 0, N_MM, "g4")
+        soft = held.tile([P, BLOCKS, NQ], F32, name="soft", tag="raw10")
+        close_groups(accs, 0, groups)
         quantise(1, 0, 0)
-        quantise(1, 0, N_MM)
-        by_columns = [(c, n0) for n0 in range(0, HALF, N_MM) for c in range(BLOCKS)]
-        accs = open_groups(1, by_columns)
+        first = [(c, 0) for c in range(BLOCKS)]
+        second = [(c, N_MM) for c in range(BLOCKS)]
+        accs = open_groups(1, first)
         interleave(on_vector, 1, 1, 0, "g5")
-        interleave(on_scalar, 1, 1, N_MM, "g6")
+        interleave(on_vector, 1, 1, N_MM, "g6")
         quantise(1, 1, 0)
+        close_groups(accs, 1, first)
+        late_codes = held.tile([P, N_MM], U32, name="late_codes", tag="g5", align_bytes=64)
+        quantise(1, 0, N_MM, late_codes)
         quantise(1, 1, N_MM)
         votes = held.tile([P, BLOCKS, NQ // SEG], F32, name="votes", tag="g4", align_bytes=64)
         for c in range(BLOCKS):
             count(c, c + 1, 0, HALF)
-        close_groups(accs, 1, by_columns)
+        accs = open_groups(1, second)
+        close_groups(accs, 1, second)
         count(0, BLOCKS, HALF, HALF + N_MM)
         for c in range(BLOCKS):
-            count(c, c + 1, HALF + N_MM, NQ)
+            if c < BLOCKS - FUSED:
+                count(c, c + 1, HALF + N_MM, NQ)
             nc.sync.dma_start(out[0, c * P : (c + 1) * P, :], votes[:, c, :])

@@ -9,13 +9,12 @@ K_PASS = P * PACK
 D, T, SLOTS, NQ, SEG = 1024, 2048, 512, 512, 32
 PASSES = D // K_PASS
 BLOCKS = SLOTS // P
-HALF = 256
-HALVES = NQ // HALF
 N_MM = 128
+PIECES = NQ // N_MM
 SHARP = 4.0
 LIVE = 96
-PIECE = 256
-FUSED = 2
+TT_ROW = P - 1
+HALF_LIST = SLOTS // 2
 
 F32 = mybir.dt.float32
 BF16 = mybir.dt.bfloat16
@@ -39,36 +38,38 @@ def tile_attend_tok_votets_topk_kernel(tc, qT, k_words, k_scales, tt, offs, out)
 
         offsets = held.tile([P, SLOTS // 16], U16, name="offsets")
         nc.sync.dma_start(offsets[:], offs)
-
         scale_pool = held.tile([P, T], U8, name="scale_pool", align_bytes=64)
         nc.sync.dma_start(
             scale_pool[LIVE:P, :].bitcast(I32), k_scales.rearrange("o f t -> f o t").bitcast(I32)
         )
-        tt_pool = held.tile([P, T], F32, name="tt_pool", tag="tt_then_codes", align_bytes=64)
-        nc.vector.memset(tt_pool[:].bitcast(I32), 0)
-        nc.vector.memset(scale_pool[0:LIVE, :].bitcast(I32), 0)
-
-        ident = held.tile([P, P], F32, name="ident")
-        make_identity(nc, ident[:])
-        warm_out = held.tile([P, 8], F32, name="warm_out")
-        nc.scalar.activation(warm_out[:], ident[:, 0:8], ACT.Sigmoid)
-        key_scales = held.tile([P, PASSES, SLOTS], U8, name="key_scales", align_bytes=64)
-        nc.gpsimd.memset(key_scales[:].rearrange("p o n -> p (o n)").bitcast(I32), 0)
-
-        raw = {}
-
-        def load_chunk(h, o):
-            raw[h, o] = held.tile([P, PACK, HALF], F32, name="raw", tag="raw%d%d" % (h, o))
-            rows = qT[0, o * K_PASS : (o + 1) * K_PASS, h * HALF : (h + 1) * HALF]
-            nc.sync.dma_start(raw[h, o][:], rows.rearrange("(p j) w -> p j w", j=PACK))
-
-        load_chunk(0, 0)
-        nc.sync.dma_start(tt_pool[0:1, :], tt[0:1, :])
+        tt_pool = held.tile([P, T], F32, name="tt_pool", align_bytes=64)
+        nc.sync.dma_start(tt_pool[TT_ROW:P, :], tt[0:1, :])
         word_pool = held.tile([P, T], U32, name="word_pool", align_bytes=64)
         nc.sync.dma_start(
             word_pool[:].bitcast(I32), k_words[0].rearrange("p t b -> p (t b)").bitcast(I32)
         )
-        load_chunk(0, 1)
+        nc.vector.memset(scale_pool[0:LIVE, :].bitcast(I32), 0)
+
+        warm = held.tile([P, 16], F32, name="warm")
+        nc.gpsimd.memset(warm[:, 0:8], 0.0)
+        nc.scalar.activation(warm[:, 8:16], warm[:, 0:8], ACT.Sigmoid)
+        nc.gpsimd.memset(tt_pool[0:TT_ROW, :].bitcast(I32), 0)
+        key_scales = held.tile([P, PASSES, SLOTS], U8, name="key_scales", align_bytes=64)
+        nc.vector.memset(key_scales[:].rearrange("p o n -> p (o n)").bitcast(I32), 0)
+        ident = held.tile([P, P], F32, name="ident")
+        make_identity(nc, ident[:])
+
+        raw = {}
+
+        def load_queries(o, n0, n1):
+            tile = held.tile([P, PACK, (n1 - n0) * N_MM], F32, name="raw", tag="raw%d%d" % (n0, o), align_bytes=64)
+            rows = qT[0, o * K_PASS : (o + 1) * K_PASS, n0 * N_MM : n1 * N_MM]
+            nc.sync.dma_start(tile[:], rows.rearrange("(p j) w -> p j w", j=PACK))
+            for n in range(n0, n1):
+                raw[n, o] = tile[:, :, (n - n0) * N_MM : (n - n0 + 1) * N_MM]
+
+        for o in range(PASSES):
+            load_queries(o, 0, 1)
 
         picked_scales = held.tile([P, SLOTS], U8, name="picked_scales", align_bytes=64)
         nc.vector.tensor_copy(picked_scales[:], scale_pool[:].indirect(offsets[:]))
@@ -77,97 +78,92 @@ def tile_attend_tok_votets_topk_kernel(tc, qT, k_words, k_scales, tt, offs, out)
                 key_scales[32 * quad : 32 * quad + 4].rearrange("p o n -> p (o n)").bitcast(I32),
                 picked_scales[LIVE + 8 * quad : LIVE + 8 * quad + 8, :].bitcast(I32),
             )
-        load_chunk(1, 0)
-        load_chunk(1, 1)
+        for n in range(1, PIECES):
+            for o in range(PASSES):
+                load_queries(o, n, n + 1)
 
         picked_tt = held.tile([P, SLOTS], F32, name="picked_tt")
         nc.vector.tensor_copy(picked_tt[:], tt_pool[:].indirect(offsets[:]))
 
         picked_words = held.tile([P, SLOTS], U32, name="picked_words", align_bytes=64)
-        key_words = held.tile([P, PASSES, SLOTS], U16, name="key_words", align_bytes=64)
-        for s0 in range(0, SLOTS, PIECE):
-            piece = picked_words[:, s0 : s0 + PIECE]
-            nc.vector.tensor_copy(piece, word_pool[:].indirect(offsets[:, s0 // 16 : (s0 + PIECE) // 16]))
+        for s0 in range(0, SLOTS, HALF_LIST):
             nc.vector.tensor_copy(
-                key_words[:, :, s0 : s0 + PIECE], piece.bitcast(U16).rearrange("p (n o) -> p o n", o=PASSES)
+                picked_words[:, s0 : s0 + HALF_LIST],
+                word_pool[:].indirect(offsets[:, s0 // 16 : (s0 + HALF_LIST) // 16]),
             )
+        key_words = {}
+
+        def part_words(half, tag):
+            s0 = half * HALF_LIST
+            key_words[half] = held.tile([P, PASSES, HALF_LIST], U16, name="key_words", tag=tag, align_bytes=64)
+            nc.vector.tensor_copy(
+                key_words[half][:],
+                picked_words[:, s0 : s0 + HALF_LIST].bitcast(U16).rearrange("p (n o) -> p o n", o=PASSES),
+            )
+
+        part_words(0, "words0")
 
         turned = psum.tile([P, BLOCKS, P], F32, name="turned", tag="bank")
         for c in range(BLOCKS):
             nc.tensor.transpose(turned[:, c, :], picked_tt[:, c * P : (c + 1) * P], ident[:])
         bias = held.tile([P, BLOCKS], F32, name="bias")
-        nc.scalar.activation(bias[:], turned[:, :, 0], ACT.Copy, scale=-SHARP)
+        nc.scalar.activation(bias[:], turned[:, :, TT_ROW], ACT.Copy, scale=-SHARP)
 
-        q_codes = held.tile([P, PASSES, NQ], U32, name="q_codes", tag="tt_then_codes", align_bytes=64)
-        q_scales = held.tile([P, PASSES, NQ], U8, name="q_scales", align_bytes=64)
+        q_codes = held.tile([P, PIECES, PASSES, N_MM], U32, name="q_codes", align_bytes=64)
+        q_scales = held.tile([P, PIECES, PASSES, N_MM], U8, name="q_scales", align_bytes=64)
+        grouped = held.tile([P, PIECES, PASSES, N_MM * PACK], BF16, name="grouped", align_bytes=64)
+        accs = {}
 
-        groups = [(c, n0) for c in range(BLOCKS) for n0 in range(0, HALF, N_MM)]
-
-        grouped = {}
-
-        def interleave(copy, h, o, n0, tag):
-            grouped[h, o, n0] = held.tile([P, N_MM, PACK], BF16, name="grouped", tag=tag, align_bytes=64)
+        def interleave(copy, n, o):
             copy(
-                grouped[h, o, n0][:].rearrange("p (c i) t -> p c t i", i=4),
-                raw[h, o][:, :, n0 : n0 + N_MM].rearrange("p t (c i) -> p c t i", i=4),
+                grouped[:, n, o, :].rearrange("p (c i t) -> p c t i", i=4, t=PACK),
+                raw[n, o].rearrange("p t (c i) -> p c t i", i=4),
             )
 
-        codes = {}
-
-        def quantise(h, o, n0, own_tile=None):
-            cols = slice(h * HALF + n0, h * HALF + n0 + N_MM)
-            codes[h, o, n0] = q_codes[:, o, cols] if own_tile is None else own_tile[:]
+        def quantise(n, o0, o1):
             nc.vector.quantize_mx(
-                out=codes[h, o, n0].bitcast(FP8X4),
-                scales=q_scales[:, o, cols],
-                in_=grouped[h, o, n0][:].rearrange("p w t -> p (w t)"),
+                out=q_codes[:, n, o0:o1, :].rearrange("p o w -> p (o w)").bitcast(FP8X4),
+                scales=q_scales[:, n, o0:o1, :].rearrange("p o w -> p (o w)"),
+                in_=grouped[:, n, o0:o1, :].rearrange("p o w -> p (o w)"),
             )
 
-        def multiply(acc, h, o, c, n0):
-            slots = slice(c * P, (c + 1) * P)
-            cols = slice(h * HALF + n0, h * HALF + n0 + N_MM)
+        def multiply(n, c, o):
+            half, s0 = divmod(c * P, HALF_LIST)
             nc.tensor.matmul_mx(
-                out=acc[:],
-                lhsT=key_words[:, o, slots].bitcast(FP4X4),
-                lhsT_scale=key_scales[:, o, slots],
-                rhs=codes[h, o, n0].bitcast(FP8X4),
-                rhs_scale=q_scales[:, o, cols],
+                out=accs[n, c],
+                lhsT=key_words[half][:, o, s0 : s0 + P].bitcast(FP4X4),
+                lhsT_scale=key_scales[:, o, c * P : (c + 1) * P],
+                rhs=q_codes[:, n, o, :].bitcast(FP8X4),
+                rhs_scale=q_scales[:, n, o, :],
                 start=(o == 0),
                 stop=(o == PASSES - 1),
             )
 
-        def open_groups(h, order):
-            accs = {}
-            for c, n0 in order:
-                accs[c, n0] = psum.tile([P, N_MM], F32, name="acc", tag="bank")
-                multiply(accs[c, n0], h, 0, c, n0)
-            return accs
+        def multiply_both(n):
+            for c in range(BLOCKS):
+                for o in range(PASSES):
+                    multiply(n, c, o)
 
-        def close_groups(accs, h, order):
-            for c, n0 in order:
-                multiply(accs[c, n0], h, 1, c, n0)
-                q0 = h * HALF + n0
-                if q0 + N_MM == NQ and c >= BLOCKS - FUSED:
-                    for r0 in range(0, N_MM, SEG):
-                        run = (q0 + r0) // SEG
-                        nc.scalar.activation(
-                            soft[:, c, q0 + r0 : q0 + r0 + SEG],
-                            accs[c, n0][:, r0 : r0 + SEG],
-                            ACT.Sigmoid,
-                            bias=bias[:, c : c + 1],
-                            scale=SHARP,
-                            accum_out=votes[:, c, run : run + 1],
-                        )
-                else:
-                    nc.scalar.activation(
-                        soft[:, c, q0 : q0 + N_MM],
-                        accs[c, n0][:],
-                        ACT.Sigmoid,
-                        bias=bias[:, c : c + 1],
-                        scale=SHARP,
-                    )
+        banks = {}
 
-        def count(c0, c1, q0, q1):
+        def take_banks(n0, n1):
+            for c in range(BLOCKS):
+                banks[n0, c] = psum.tile([P, (n1 - n0) * N_MM], F32, name="acc", tag="bank")
+                for n in range(n0, n1):
+                    accs[n, c] = banks[n0, c][:, (n - n0) * N_MM : (n - n0 + 1) * N_MM]
+
+        def soften(n0, n1):
+            for c in range(BLOCKS):
+                nc.scalar.activation(
+                    soft[:, c, n0 * N_MM : n1 * N_MM],
+                    banks[n0, c][:],
+                    ACT.Sigmoid,
+                    bias=bias[:, c : c + 1],
+                    scale=SHARP,
+                )
+
+        def count(c0, c1, n0, n1):
+            q0, q1 = n0 * N_MM, n1 * N_MM
             nc.vector.tensor_reduce(
                 votes[:, c0:c1, q0 // SEG : q1 // SEG],
                 soft[:, c0:c1, q0:q1].rearrange("p c (j r) -> p c j r", r=SEG),
@@ -176,37 +172,34 @@ def tile_attend_tok_votets_topk_kernel(tc, qT, k_words, k_scales, tt, offs, out)
             )
 
         on_scalar, on_vector = nc.scalar.copy, nc.vector.tensor_copy
-        interleave(on_scalar, 0, 0, 0, "g0")
-        interleave(on_scalar, 0, 0, N_MM, "g1")
-        quantise(0, 0, 0)
-        quantise(0, 0, N_MM)
-        accs = open_groups(0, groups)
-        interleave(on_scalar, 0, 1, 0, "g2")
-        interleave(on_scalar, 0, 1, N_MM, "g7")
-        quantise(0, 1, 0)
-        quantise(0, 1, N_MM)
-        interleave(on_scalar, 1, 0, 0, "g3")
-        interleave(on_vector, 1, 0, N_MM, "g4")
-        soft = held.tile([P, BLOCKS, NQ], F32, name="soft", tag="raw10")
-        close_groups(accs, 0, groups)
-        quantise(1, 0, 0)
-        first = [(c, 0) for c in range(BLOCKS)]
-        second = [(c, N_MM) for c in range(BLOCKS)]
-        accs = open_groups(1, first)
-        interleave(on_vector, 1, 1, 0, "g5")
-        interleave(on_vector, 1, 1, N_MM, "g6")
-        quantise(1, 1, 0)
-        close_groups(accs, 1, first)
-        late_codes = held.tile([P, N_MM], U32, name="late_codes", tag="g5", align_bytes=64)
-        quantise(1, 0, N_MM, late_codes)
-        quantise(1, 1, N_MM)
-        votes = held.tile([P, BLOCKS, NQ // SEG], F32, name="votes", tag="g4", align_bytes=64)
-        for c in range(BLOCKS):
-            count(c, c + 1, 0, HALF)
-        accs = open_groups(1, second)
-        close_groups(accs, 1, second)
-        count(0, BLOCKS, HALF, HALF + N_MM)
-        for c in range(BLOCKS):
-            if c < BLOCKS - FUSED:
-                count(c, c + 1, HALF + N_MM, NQ)
-            nc.sync.dma_start(out[0, c * P : (c + 1) * P, :], votes[:, c, :])
+        interleave(on_scalar, 0, 0)
+        interleave(on_scalar, 0, 1)
+        quantise(0, 0, 2)
+        part_words(1, "raw01")
+        interleave(on_scalar, 1, 0)
+        interleave(on_scalar, 1, 1)
+        quantise(1, 0, 2)
+        interleave(on_scalar, 2, 0)
+        soft = held.tile([P, BLOCKS, NQ], F32, name="soft", tag="raw20", align_bytes=64)
+        interleave(on_vector, 2, 1)
+        quantise(2, 0, 2)
+        for n in range(PIECES - 1):
+            take_banks(n, n + 1)
+            multiply_both(n)
+            soften(n, n + 1)
+        interleave(on_vector, 3, 0)
+        quantise(3, 0, 1)
+        interleave(on_vector, 3, 1)
+        votes = held.tile([P, BLOCKS, NQ // SEG], F32, name="votes", tag="raw31", align_bytes=64)
+        quantise(3, 1, 2)
+        take_banks(3, 4)
+        for o in range(PASSES):
+            for c in range(BLOCKS):
+                multiply(3, c, o)
+        soften(3, 4)
+        count(0, BLOCKS, 0, 2)
+        count(0, BLOCKS, 2, 3)
+        count(0, 2, 3, 4)
+        nc.sync.dma_start(out[0, 0 : 2 * P, :].rearrange("(c p) j -> p c j", p=P), votes[:, 0:2, :])
+        count(2, 4, 3, 4)
+        nc.sync.dma_start(out[0, 2 * P : 4 * P, :].rearrange("(c p) j -> p c j", p=P), votes[:, 2:4, :])

@@ -15,6 +15,8 @@ SHARP = 4.0
 LIVE = 96
 TT_ROW = P - 1
 HALF_LIST = SLOTS // 2
+FUSED = 1
+AHEAD = 3
 
 F32 = mybir.dt.float32
 BF16 = mybir.dt.bfloat16
@@ -38,7 +40,7 @@ def tile_attend_tok_votets_topk_kernel(tc, qT, k_words, k_scales, tt, offs, out)
 
         offsets = held.tile([P, SLOTS // 16], U16, name="offsets")
         nc.sync.dma_start(offsets[:], offs)
-        scale_pool = held.tile([P, T], U8, name="scale_pool", align_bytes=64)
+        scale_pool = held.tile([P, T], U8, name="scale_pool", tag="scales", align_bytes=64)
         nc.sync.dma_start(
             scale_pool[LIVE:P, :].bitcast(I32), k_scales.rearrange("o f t -> f o t").bitcast(I32)
         )
@@ -50,14 +52,11 @@ def tile_attend_tok_votets_topk_kernel(tc, qT, k_words, k_scales, tt, offs, out)
         )
         nc.vector.memset(scale_pool[0:LIVE, :].bitcast(I32), 0)
 
-        warm = held.tile([P, 16], F32, name="warm")
-        nc.gpsimd.memset(warm[:, 0:8], 0.0)
-        nc.scalar.activation(warm[:, 8:16], warm[:, 0:8], ACT.Sigmoid)
-        nc.gpsimd.memset(tt_pool[0:TT_ROW, :].bitcast(I32), 0)
-        key_scales = held.tile([P, PASSES, SLOTS], U8, name="key_scales", align_bytes=64)
-        nc.vector.memset(key_scales[:].rearrange("p o n -> p (o n)").bitcast(I32), 0)
+        nc.vector.memset(tt_pool[0:TT_ROW, :].bitcast(I32), 0)
         ident = held.tile([P, P], F32, name="ident")
         make_identity(nc, ident[:])
+        warm = held.tile([P, 8], F32, name="warm")
+        nc.scalar.activation(warm[:], ident[:, 0:8], ACT.Sigmoid)
 
         raw = {}
 
@@ -68,19 +67,20 @@ def tile_attend_tok_votets_topk_kernel(tc, qT, k_words, k_scales, tt, offs, out)
             for n in range(n0, n1):
                 raw[n, o] = tile[:, :, (n - n0) * N_MM : (n - n0 + 1) * N_MM]
 
-        for o in range(PASSES):
-            load_queries(o, 0, 1)
+        pieces = [(n, o) for n in range(PIECES) for o in range(PASSES)]
+        for n, o in pieces[:AHEAD]:
+            load_queries(o, n, n + 1)
 
         picked_scales = held.tile([P, SLOTS], U8, name="picked_scales", align_bytes=64)
         nc.vector.tensor_copy(picked_scales[:], scale_pool[:].indirect(offsets[:]))
+        key_scales = held.tile([P, PASSES, SLOTS], U8, name="key_scales", tag="scales", align_bytes=64)
         for quad in range(4):
             nc.sync.dma_start(
                 key_scales[32 * quad : 32 * quad + 4].rearrange("p o n -> p (o n)").bitcast(I32),
                 picked_scales[LIVE + 8 * quad : LIVE + 8 * quad + 8, :].bitcast(I32),
             )
-        for n in range(1, PIECES):
-            for o in range(PASSES):
-                load_queries(o, n, n + 1)
+        for n, o in pieces[AHEAD:]:
+            load_queries(o, n, n + 1)
 
         picked_tt = held.tile([P, SLOTS], F32, name="picked_tt")
         nc.vector.tensor_copy(picked_tt[:], tt_pool[:].indirect(offsets[:]))
@@ -152,54 +152,80 @@ def tile_attend_tok_votets_topk_kernel(tc, qT, k_words, k_scales, tt, offs, out)
                 for n in range(n0, n1):
                     accs[n, c] = banks[n0, c][:, (n - n0) * N_MM : (n - n0 + 1) * N_MM]
 
-        def soften(n0, n1):
-            for c in range(BLOCKS):
+        def soften(n0, n1, blocks=BLOCKS):
+            for c in range(blocks):
                 nc.scalar.activation(
-                    soft[:, c, n0 * N_MM : n1 * N_MM],
+                    soft[n0][:, c, :],
                     banks[n0, c][:],
                     ACT.Sigmoid,
                     bias=bias[:, c : c + 1],
                     scale=SHARP,
                 )
 
-        def count(c0, c1, n0, n1):
-            q0, q1 = n0 * N_MM, n1 * N_MM
+        soft = {}
+        runs = N_MM // SEG
+
+        def count(c0, c1, n):
             nc.vector.tensor_reduce(
-                votes[:, c0:c1, q0 // SEG : q1 // SEG],
-                soft[:, c0:c1, q0:q1].rearrange("p c (j r) -> p c j r", r=SEG),
+                votes[:, c0:c1, n * runs : (n + 1) * runs],
+                soft[n][:, c0:c1, :].rearrange("p c (j r) -> p c j r", r=SEG),
                 mybir.AxisListType.X,
                 mybir.AluOpType.add,
             )
 
         on_scalar, on_vector = nc.scalar.copy, nc.vector.tensor_copy
+        def scores(n, tag):
+            soft[n] = held.tile([P, BLOCKS, N_MM], F32, name="soft", tag=tag, align_bytes=64)
+            take_banks(n, n + 1)
+            multiply_both(n)
+            soften(n, n + 1)
+
+        def store(c0, c1):
+            rows = out[0, c0 * P : c1 * P, :]
+            nc.sync.dma_start(rows.rearrange("(c p) j -> p c j", p=P), votes[:, c0:c1, :])
+
+        def soften_and_count(n, c):
+            for j in range(runs):
+                nc.scalar.activation(
+                    soft[n][:, c, j * SEG : (j + 1) * SEG],
+                    banks[n, c][:, j * SEG : (j + 1) * SEG],
+                    ACT.Sigmoid,
+                    bias=bias[:, c : c + 1],
+                    scale=SHARP,
+                    accum_out=votes[:, c, n * runs + j : n * runs + j + 1],
+                )
+
         interleave(on_scalar, 0, 0)
         interleave(on_scalar, 0, 1)
         quantise(0, 0, 2)
         part_words(1, "raw01")
         interleave(on_scalar, 1, 0)
-        interleave(on_scalar, 1, 1)
+        interleave(on_vector, 1, 1)
         quantise(1, 0, 2)
-        interleave(on_scalar, 2, 0)
-        soft = held.tile([P, BLOCKS, NQ], F32, name="soft", tag="raw20", align_bytes=64)
-        interleave(on_vector, 2, 1)
-        quantise(2, 0, 2)
-        for n in range(PIECES - 1):
-            take_banks(n, n + 1)
-            multiply_both(n)
-            soften(n, n + 1)
+        scores(0, "soft0")
+        interleave(on_vector, 2, 0)
+        votes = held.tile([P, BLOCKS, NQ // SEG], F32, name="votes", tag="raw20", align_bytes=64)
+        interleave(on_scalar, 2, 1)
+        count(0, 2, 0)
+        count(2, 4, 0)
         interleave(on_vector, 3, 0)
-        quantise(3, 0, 1)
+        quantise(2, 0, 2)
         interleave(on_vector, 3, 1)
-        votes = held.tile([P, BLOCKS, NQ // SEG], F32, name="votes", tag="raw31", align_bytes=64)
-        quantise(3, 1, 2)
+        quantise(3, 0, 2)
+        scores(1, "raw21")
+        scores(2, "soft2")
+        soft[3] = held.tile([P, BLOCKS, N_MM], F32, name="soft", tag="soft3", align_bytes=64)
         take_banks(3, 4)
-        for o in range(PASSES):
-            for c in range(BLOCKS):
-                multiply(3, c, o)
-        soften(3, 4)
-        count(0, BLOCKS, 0, 2)
-        count(0, BLOCKS, 2, 3)
-        count(0, 2, 3, 4)
-        nc.sync.dma_start(out[0, 0 : 2 * P, :].rearrange("(c p) j -> p c j", p=P), votes[:, 0:2, :])
-        count(2, 4, 3, 4)
-        nc.sync.dma_start(out[0, 2 * P : 4 * P, :].rearrange("(c p) j -> p c j", p=P), votes[:, 2:4, :])
+        multiply_both(3)
+        plain = BLOCKS - FUSED
+        soften(3, 4, plain)
+        for c in range(plain, BLOCKS):
+            soften_and_count(3, c)
+        count(0, 2, 1)
+        count(2, 4, 1)
+        count(0, 4, 2)
+        count(0, 2, 3)
+        store(0, 2)
+        if plain > 2:
+            count(2, plain, 3)
+        store(2, 4)

@@ -106,8 +106,6 @@ def tile_attend_tok_votets_topk_kernel(tc, qT, k_words, k_scales, tt, offs, out)
         turned = psum.tile([P, BLOCKS, P], F32, name="turned", tag="bank")
         for c in range(BLOCKS):
             nc.tensor.transpose(turned[:, c, :], picked_tt[:, c * P : (c + 1) * P], ident[:])
-        bias = held.tile([P, BLOCKS], F32, name="bias")
-        nc.scalar.activation(bias[:], turned[:, :, TT_ROW], ACT.Copy, scale=-SHARP)
 
         q_codes = held.tile([P, PIECES, PASSES, N_MM], U32, name="q_codes", align_bytes=64)
         q_scales = held.tile([P, PIECES, PASSES, N_MM], U8, name="q_scales", align_bytes=64)
@@ -202,6 +200,8 @@ def tile_attend_tok_votets_topk_kernel(tc, qT, k_words, k_scales, tt, offs, out)
         interleave(on_scalar, 1, 0)
         interleave(on_vector, 1, 1)
         quantise(1, 0, 2)
+        bias = held.tile([P, BLOCKS], F32, name="bias", tag="raw10", align_bytes=64)
+        nc.scalar.activation(bias[:], turned[:, :, TT_ROW], ACT.Copy, scale=-SHARP)
         scores(0, "soft0")
         interleave(on_vector, 2, 0)
         votes = held.tile([P, BLOCKS, NQ // SEG], F32, name="votes", tag="raw20", align_bytes=64)

@@ -38,12 +38,12 @@ def tile_attend_tok_votets_topk_kernel(tc, qT, k_words, k_scales, tt, offs, out)
         held = ctx.enter_context(tc.tile_pool(name="held", bufs=1))
         psum = ctx.enter_context(tc.psum_pool(name="psum", bufs=8))
 
-        offsets = held.tile([P, SLOTS // 16], U16, name="offsets")
-        nc.sync.dma_start(offsets[:], offs)
         scale_pool = held.tile([P, T], U8, name="scale_pool", tag="scales", align_bytes=64)
         nc.sync.dma_start(
             scale_pool[LIVE:P, :].bitcast(I32), k_scales.rearrange("o f t -> f o t").bitcast(I32)
         )
+        offsets = held.tile([P, SLOTS // 16], U16, name="offsets")
+        nc.sync.dma_start(offsets[:], offs)
         tt_pool = held.tile([P, T], F32, name="tt_pool", align_bytes=64)
         nc.sync.dma_start(tt_pool[TT_ROW:P, :], tt[0:1, :])
         word_pool = held.tile([P, T], U32, name="word_pool", align_bytes=64)
@@ -74,7 +74,7 @@ def tile_attend_tok_votets_topk_kernel(tc, qT, k_words, k_scales, tt, offs, out)
         picked_scales = held.tile([P, SLOTS], U8, name="picked_scales", align_bytes=64)
         nc.vector.tensor_copy(picked_scales[:], scale_pool[:].indirect(offsets[:]))
         key_scales = held.tile([P, PASSES, SLOTS], U8, name="key_scales", tag="scales", align_bytes=64)
-        for quad in range(4):
+        for quad in (0, 2, 1, 3):
             nc.sync.dma_start(
                 key_scales[32 * quad : 32 * quad + 4].rearrange("p o n -> p (o n)").bitcast(I32),
                 picked_scales[LIVE + 8 * quad : LIVE + 8 * quad + 8, :].bitcast(I32),
@@ -210,13 +210,16 @@ def tile_attend_tok_votets_topk_kernel(tc, qT, k_words, k_scales, tt, offs, out)
         count(2, 4, 0)
         interleave(on_vector, 3, 0)
         quantise(2, 0, 2)
+        quantise(3, 0, 1)
         interleave(on_vector, 3, 1)
-        quantise(3, 0, 2)
+        quantise(3, 1, 2)
         scores(1, "raw21")
         scores(2, "soft2")
         soft[3] = held.tile([P, BLOCKS, N_MM], F32, name="soft", tag="soft3", align_bytes=64)
         take_banks(3, 4)
-        multiply_both(3)
+        for o in range(PASSES):
+            for c in range(BLOCKS):
+                multiply(3, c, o)
         plain = BLOCKS - FUSED
         soften(3, 4, plain)
         for c in range(plain, BLOCKS):

@@ -15,6 +15,8 @@ SHARP = 4.0
 LIVE = 96
 TT_ROW = P - 1
 HALF_LIST = SLOTS // 2
+SEED = 16
+COPIED = 800
 FUSED = 1
 AHEAD = 3
 
@@ -45,18 +47,26 @@ def tile_attend_tok_votets_topk_kernel(tc, qT, k_words, k_scales, tt, offs, out)
         offsets = held.tile([P, SLOTS // 16], U16, name="offsets")
         nc.sync.dma_start(offsets[:], offs)
         tt_pool = held.tile([P, T], F32, name="tt_pool", align_bytes=64)
+        tt_seed = held.tile([P, SEED], F32, name="tt_seed")
+        nc.sync.dma_start(tt_seed[:], tt[:, 0:SEED])
         nc.sync.dma_start(tt_pool[TT_ROW:P, :], tt[0:1, :])
         word_pool = held.tile([P, T], U32, name="word_pool", align_bytes=64)
         nc.sync.dma_start(
             word_pool[:].bitcast(I32), k_words[0].rearrange("p t b -> p (t b)").bitcast(I32)
         )
+        warm = held.tile([P, 16], F32, name="warm")
+        nc.vector.memset(warm[:, 0:8], 0.0)
+        nc.scalar.activation(warm[:, 8:16], warm[:, 0:8], ACT.Sigmoid)
         nc.vector.memset(scale_pool[0:LIVE, :].bitcast(I32), 0)
 
-        nc.vector.memset(tt_pool[0:TT_ROW, :].bitcast(I32), 0)
+        nc.vector.memset(tt_pool[0:TT_ROW, COPIED:T].bitcast(I32), 0)
+        nc.scalar.activation(
+            tt_pool[0:TT_ROW, 0:COPIED].rearrange("p (a b) -> p a b", b=SEED),
+            tt_seed[0:TT_ROW, :].unsqueeze(1).to_broadcast([TT_ROW, COPIED // SEED, SEED]),
+            ACT.Copy,
+        )
         ident = held.tile([P, P], F32, name="ident")
         make_identity(nc, ident[:])
-        warm = held.tile([P, 8], F32, name="warm")
-        nc.scalar.activation(warm[:], ident[:, 0:8], ACT.Sigmoid)
 
         raw = {}
 

@@ -49,7 +49,7 @@ def tile_attend_tok_votets_topk_kernel(tc, qT, k_words, k_scales, tt, offs, out)
         tt_pool = held.tile([P, T], F32, name="tt_pool", align_bytes=64)
         tt_seed = held.tile([P, SEED], F32, name="tt_seed")
         nc.sync.dma_start(tt_seed[:], tt[:, 0:SEED])
-        nc.sync.dma_start(tt_pool[TT_ROW:P, :], tt[0:1, :])
+        nc.scalar.dma_start(tt_pool[TT_ROW:P, :], tt[0:1, :])
         word_pool = held.tile([P, T], U32, name="word_pool", align_bytes=64)
         nc.sync.dma_start(
             word_pool[:].bitcast(I32), k_words[0].rearrange("p t b -> p (t b)").bitcast(I32)

@@ -16,7 +16,7 @@ LIVE = 96
 TT_ROW = P - 1
 HALF_LIST = SLOTS // 2
 SEED = 16
-COPIED = 800
+COPIED = 704
 FUSED = 1
 AHEAD = 3
 
@@ -55,7 +55,7 @@ def tile_attend_tok_votets_topk_kernel(tc, qT, k_words, k_scales, tt, offs, out)
             word_pool[:].bitcast(I32), k_words[0].rearrange("p t b -> p (t b)").bitcast(I32)
         )
         warm = held.tile([P, 16], F32, name="warm")
-        nc.vector.memset(warm[:, 0:8], 0.0)
+        nc.gpsimd.memset(warm[:, 0:8], 0.0)
         nc.scalar.activation(warm[:, 8:16], warm[:, 0:8], ACT.Sigmoid)
         nc.vector.memset(scale_pool[0:LIVE, :].bitcast(I32), 0)
 

@@ -18,7 +18,7 @@ HALF_LIST = SLOTS // 2
 SEED = 16
 COPIED = 704
 FUSED = 1
-AHEAD = 3
+AHEAD = 2
 
 F32 = mybir.dt.float32
 BF16 = mybir.dt.bfloat16

@@ -15,8 +15,6 @@ SHARP = 4.0
 LIVE = 96
 TT_ROW = P - 1
 HALF_LIST = SLOTS // 2
-SEED = 16
-COPIED = 704
 FUSED = 1
 AHEAD = 2
 
@@ -47,8 +45,6 @@ def tile_attend_tok_votets_topk_kernel(tc, qT, k_words, k_scales, tt, offs, out)
         offsets = held.tile([P, SLOTS // 16], U16, name="offsets")
         nc.sync.dma_start(offsets[:], offs)
         tt_pool = held.tile([P, T], F32, name="tt_pool", align_bytes=64)
-        tt_seed = held.tile([P, SEED], F32, name="tt_seed")
-        nc.sync.dma_start(tt_seed[:], tt[:, 0:SEED])
         nc.scalar.dma_start(tt_pool[TT_ROW:P, :], tt[0:1, :])
         word_pool = held.tile([P, T], U32, name="word_pool", align_bytes=64)
         nc.sync.dma_start(
@@ -59,14 +55,10 @@ def tile_attend_tok_votets_topk_kernel(tc, qT, k_words, k_scales, tt, offs, out)
         nc.scalar.activation(warm[:, 8:16], warm[:, 0:8], ACT.Sigmoid)
         nc.vector.memset(scale_pool[0:LIVE, :].bitcast(I32), 0)
 
-        nc.vector.memset(tt_pool[0:TT_ROW, COPIED:T].bitcast(I32), 0)
-        nc.scalar.activation(
-            tt_pool[0:TT_ROW, 0:COPIED].rearrange("p (a b) -> p a b", b=SEED),
-            tt_seed[0:TT_ROW, :].unsqueeze(1).to_broadcast([TT_ROW, COPIED // SEED, SEED]),
-            ACT.Copy,
-        )
         ident = held.tile([P, P], F32, name="ident")
-        make_identity(nc, ident[:])
+        nc.vector.memset(ident[:], 0.0)
+        nc.vector.memset(tt_pool[0:TT_ROW, :].bitcast(I32), 0)
+        make_identity(nc, ident[:], nomemset=True)
 
         raw = {}
 

@@ -11,12 +11,11 @@ PASSES = D // K_PASS
 BLOCKS = SLOTS // P
 N_MM = 128
 PIECES = NQ // N_MM
+RUNS = N_MM // SEG
 SHARP = 4.0
 LIVE = 96
 TT_ROW = P - 1
 HALF_LIST = SLOTS // 2
-FUSED = 1
-AHEAD = 2
 
 F32 = mybir.dt.float32
 BF16 = mybir.dt.bfloat16
@@ -31,12 +30,13 @@ ACT = mybir.ActivationFunctionType
 FLOPS = 2 * SLOTS * NQ * D
 BYTES = 4 * D * NQ + P * T * 4 + PASSES * 16 * T + 4 * T + 2 * P * SLOTS // 16 + 4 * SLOTS * NQ // SEG
 
+LATE_CUTS = ((0, 2), (2, 3), (3, 4))
 
 def tile_attend_tok_votets_topk_kernel(tc, qT, k_words, k_scales, tt, offs, out):
     nc = tc.nc
     with ExitStack() as ctx:
         held = ctx.enter_context(tc.tile_pool(name="held", bufs=1))
-        psum = ctx.enter_context(tc.psum_pool(name="psum", bufs=8))
+        psum = ctx.enter_context(tc.psum_pool(name="psum", bufs=1))
 
         scale_pool = held.tile([P, T], U8, name="scale_pool", tag="scales", align_bytes=64)
         nc.sync.dma_start(
@@ -46,6 +46,16 @@ def tile_attend_tok_votets_topk_kernel(tc, qT, k_words, k_scales, tt, offs, out)
         nc.sync.dma_start(offsets[:], offs)
         tt_pool = held.tile([P, T], F32, name="tt_pool", align_bytes=64)
         nc.scalar.dma_start(tt_pool[TT_ROW:P, :], tt[0:1, :])
+        raw = {}
+
+        def load_queries(o, n0, n1):
+            tile = held.tile([P, PACK, (n1 - n0) * N_MM], F32, name="raw", tag="raw%d%d" % (n0, o), align_bytes=64)
+            rows = qT[0, o * K_PASS : (o + 1) * K_PASS, n0 * N_MM : n1 * N_MM]
+            nc.sync.dma_start(tile[:], rows.rearrange("(p j) w -> p j w", j=PACK))
+            for n in range(n0, n1):
+                raw[n, o] = tile[:, :, (n - n0) * N_MM : (n - n0 + 1) * N_MM]
+
+        load_queries(0, 0, PIECES)
         word_pool = held.tile([P, T], U32, name="word_pool", align_bytes=64)
         nc.sync.dma_start(
             word_pool[:].bitcast(I32), k_words[0].rearrange("p t b -> p (t b)").bitcast(I32)
@@ -60,19 +70,6 @@ def tile_attend_tok_votets_topk_kernel(tc, qT, k_words, k_scales, tt, offs, out)
         nc.vector.memset(tt_pool[0:TT_ROW, :].bitcast(I32), 0)
         make_identity(nc, ident[:], nomemset=True)
 
-        raw = {}
-
-        def load_queries(o, n0, n1):
-            tile = held.tile([P, PACK, (n1 - n0) * N_MM], F32, name="raw", tag="raw%d%d" % (n0, o), align_bytes=64)
-            rows = qT[0, o * K_PASS : (o + 1) * K_PASS, n0 * N_MM : n1 * N_MM]
-            nc.sync.dma_start(tile[:], rows.rearrange("(p j) w -> p j w", j=PACK))
-            for n in range(n0, n1):
-                raw[n, o] = tile[:, :, (n - n0) * N_MM : (n - n0 + 1) * N_MM]
-
-        pieces = [(n, o) for n in range(PIECES) for o in range(PASSES)]
-        for n, o in pieces[:AHEAD]:
-            load_queries(o, n, n + 1)
-
         picked_scales = held.tile([P, SLOTS], U8, name="picked_scales", align_bytes=64)
         nc.vector.tensor_copy(picked_scales[:], scale_pool[:].indirect(offsets[:]))
         key_scales = held.tile([P, PASSES, SLOTS], U8, name="key_scales", tag="scales", align_bytes=64)
@@ -81,18 +78,21 @@ def tile_attend_tok_votets_topk_kernel(tc, qT, k_words, k_scales, tt, offs, out)
                 key_scales[32 * quad : 32 * quad + 4].rearrange("p o n -> p (o n)").bitcast(I32),
                 picked_scales[LIVE + 8 * quad : LIVE + 8 * quad + 8, :].bitcast(I32),
             )
-        for n, o in pieces[AHEAD:]:
-            load_queries(o, n, n + 1)
+        for n0, n1 in LATE_CUTS:
+            load_queries(1, n0, n1)
 
         picked_tt = held.tile([P, SLOTS], F32, name="picked_tt")
         nc.vector.tensor_copy(picked_tt[:], tt_pool[:].indirect(offsets[:]))
 
         picked_words = held.tile([P, SLOTS], U32, name="picked_words", align_bytes=64)
-        for s0 in range(0, SLOTS, HALF_LIST):
+
+        def gather_words(half):
+            s0 = half * HALF_LIST
             nc.vector.tensor_copy(
                 picked_words[:, s0 : s0 + HALF_LIST],
                 word_pool[:].indirect(offsets[:, s0 // 16 : (s0 + HALF_LIST) // 16]),
             )
+
         key_words = {}
 
         def part_words(half, tag):
@@ -103,134 +103,123 @@ def tile_attend_tok_votets_topk_kernel(tc, qT, k_words, k_scales, tt, offs, out)
                 picked_words[:, s0 : s0 + HALF_LIST].bitcast(U16).rearrange("p (n o) -> p o n", o=PASSES),
             )
 
-        part_words(0, "words0")
-
-        turned = psum.tile([P, BLOCKS, P], F32, name="turned", tag="bank")
+        turned = psum.tile([P, BLOCKS, P], F32, name="turned", tag="bank7")
         for c in range(BLOCKS):
             nc.tensor.transpose(turned[:, c, :], picked_tt[:, c * P : (c + 1) * P], ident[:])
 
-        q_codes = held.tile([P, PIECES, PASSES, N_MM], U32, name="q_codes", align_bytes=64)
-        q_scales = held.tile([P, PIECES, PASSES, N_MM], U8, name="q_scales", align_bytes=64)
-        grouped = held.tile([P, PIECES, PASSES, N_MM * PACK], BF16, name="grouped", align_bytes=64)
-        accs = {}
+        q_codes = held.tile([P, PASSES, PIECES, N_MM], U32, name="q_codes", align_bytes=64)
+        q_scales = held.tile([P, PASSES, PIECES, N_MM], U8, name="q_scales", align_bytes=64)
+        grouped = held.tile([P, PASSES, PIECES, N_MM * PACK], BF16, name="grouped", align_bytes=64)
+        on_scalar, on_vector = nc.scalar.copy, nc.vector.tensor_copy
+        banks, soft, votes = {}, {}, {}
 
         def interleave(copy, n, o):
             copy(
-                grouped[:, n, o, :].rearrange("p (c i t) -> p c t i", i=4, t=PACK),
+                grouped[:, o, n, :].rearrange("p (c i t) -> p c t i", i=4, t=PACK),
                 raw[n, o].rearrange("p t (c i) -> p c t i", i=4),
             )
 
-        def quantise(n, o0, o1):
+        def quantise(o, n0, n1):
             nc.vector.quantize_mx(
-                out=q_codes[:, n, o0:o1, :].rearrange("p o w -> p (o w)").bitcast(FP8X4),
-                scales=q_scales[:, n, o0:o1, :].rearrange("p o w -> p (o w)"),
-                in_=grouped[:, n, o0:o1, :].rearrange("p o w -> p (o w)"),
+                out=q_codes[:, o, n0:n1, :].rearrange("p n w -> p (n w)").bitcast(FP8X4),
+                scales=q_scales[:, o, n0:n1, :].rearrange("p n w -> p (n w)"),
+                in_=grouped[:, o, n0:n1, :].rearrange("p n w -> p (n w)"),
             )
 
-        def multiply(n, c, o):
+        def multiply(n, c, o, first=0):
             half, s0 = divmod(c * P, HALF_LIST)
             nc.tensor.matmul_mx(
-                out=accs[n, c],
+                out=banks[n, c],
                 lhsT=key_words[half][:, o, s0 : s0 + P].bitcast(FP4X4),
                 lhsT_scale=key_scales[:, o, c * P : (c + 1) * P],
-                rhs=q_codes[:, n, o, :].bitcast(FP8X4),
-                rhs_scale=q_scales[:, n, o, :],
-                start=(o == 0),
-                stop=(o == PASSES - 1),
+                rhs=q_codes[:, o, n, :].bitcast(FP8X4),
+                rhs_scale=q_scales[:, o, n, :],
+                start=(o == first),
+                stop=(o != first),
             )
 
-        def multiply_both(n):
+        def take_banks(n, numbers):
+            shared = BLOCKS // len(numbers)
+            for i, number in enumerate(numbers):
+                bank = psum.tile([P, shared, N_MM], F32, name="acc", tag="bank%d" % number)
+                for c in range(shared):
+                    banks[n, i * shared + c] = bank[:, c, :]
+
+        def by_block(n):
             for c in range(BLOCKS):
                 for o in range(PASSES):
                     multiply(n, c, o)
 
-        banks = {}
+        def by_pass(n):
+            for o in range(PASSES):
+                for c in range(BLOCKS):
+                    multiply(n, c, o)
 
-        def take_banks(n0, n1):
-            for c in range(BLOCKS):
-                banks[n0, c] = psum.tile([P, (n1 - n0) * N_MM], F32, name="acc", tag="bank")
-                for n in range(n0, n1):
-                    accs[n, c] = banks[n0, c][:, (n - n0) * N_MM : (n - n0 + 1) * N_MM]
-
-        def soften(n0, n1, blocks=BLOCKS):
+        def soften(n, tag, blocks=BLOCKS):
+            soft[n] = held.tile([P, BLOCKS, N_MM], F32, name="soft", tag=tag, align_bytes=64)
             for c in range(blocks):
                 nc.scalar.activation(
-                    soft[n0][:, c, :],
-                    banks[n0, c][:],
-                    ACT.Sigmoid,
-                    bias=bias[:, c : c + 1],
-                    scale=SHARP,
+                    soft[n][:, c, :], banks[n, c], ACT.Sigmoid, bias=bias[:, c : c + 1], scale=SHARP
                 )
 
-        soft = {}
-        runs = N_MM // SEG
-
-        def count(c0, c1, n):
-            nc.vector.tensor_reduce(
-                votes[:, c0:c1, n * runs : (n + 1) * runs],
-                soft[n][:, c0:c1, :].rearrange("p c (j r) -> p c j r", r=SEG),
-                mybir.AxisListType.X,
-                mybir.AluOpType.add,
-            )
-
-        on_scalar, on_vector = nc.scalar.copy, nc.vector.tensor_copy
-        def scores(n, tag):
-            soft[n] = held.tile([P, BLOCKS, N_MM], F32, name="soft", tag=tag, align_bytes=64)
-            take_banks(n, n + 1)
-            multiply_both(n)
-            soften(n, n + 1)
-
-        def store(c0, c1):
-            rows = out[0, c0 * P : c1 * P, :]
-            nc.sync.dma_start(rows.rearrange("(c p) j -> p c j", p=P), votes[:, c0:c1, :])
-
         def soften_and_count(n, c):
-            for j in range(runs):
+            for j in range(RUNS):
                 nc.scalar.activation(
                     soft[n][:, c, j * SEG : (j + 1) * SEG],
                     banks[n, c][:, j * SEG : (j + 1) * SEG],
                     ACT.Sigmoid,
                     bias=bias[:, c : c + 1],
                     scale=SHARP,
-                    accum_out=votes[:, c, n * runs + j : n * runs + j + 1],
+                    accum_out=votes[c // 2][:, c % 2, n * RUNS + j : n * RUNS + j + 1],
                 )
 
-        interleave(on_scalar, 0, 0)
-        interleave(on_scalar, 0, 1)
-        quantise(0, 0, 2)
-        part_words(1, "raw01")
-        interleave(on_scalar, 1, 0)
-        interleave(on_vector, 1, 1)
-        quantise(1, 0, 2)
-        bias = held.tile([P, BLOCKS], F32, name="bias", tag="raw10", align_bytes=64)
+        def count(n, c0, c1):
+            nc.vector.tensor_reduce(
+                votes[c0 // 2][:, c0 % 2 : c0 % 2 + c1 - c0, n * RUNS : (n + 1) * RUNS],
+                soft[n][:, c0:c1, :].rearrange("p c (j r) -> p c j r", r=SEG),
+                mybir.AxisListType.X,
+                mybir.AluOpType.add,
+            )
+
+        def store(pair):
+            rows = out[0, 2 * pair * P : 2 * (pair + 1) * P, :]
+            nc.sync.dma_start(rows.rearrange("(c p) j -> p c j", p=P), votes[pair][:])
+
+        bias = held.tile([P, BLOCKS], F32, name="bias", tag="bias", align_bytes=64)
         nc.scalar.activation(bias[:], turned[:, :, TT_ROW], ACT.Copy, scale=-SHARP)
-        scores(0, "soft0")
-        interleave(on_vector, 2, 0)
-        votes = held.tile([P, BLOCKS, NQ // SEG], F32, name="votes", tag="raw20", align_bytes=64)
-        interleave(on_scalar, 2, 1)
-        count(0, 2, 0)
-        count(2, 4, 0)
+        interleave(on_scalar, 0, 0)
         interleave(on_vector, 3, 0)
-        quantise(2, 0, 2)
-        quantise(3, 0, 1)
+        interleave(on_scalar, 1, 0)
+        interleave(on_scalar, 2, 0)
+        quantise(0, 0, 2)
+        quantise(0, 2, 4)
+        gather_words(0)
+        gather_words(1)
+        part_words(0, "words0")
+        part_words(1, "words1")
+        interleave(on_scalar, 0, 1)
+        quantise(1, 0, 1)
+        interleave(on_scalar, 1, 1)
+        interleave(on_vector, 2, 1)
+        quantise(1, 1, 2)
         interleave(on_vector, 3, 1)
-        quantise(3, 1, 2)
-        scores(1, "raw21")
-        scores(2, "soft2")
-        soft[3] = held.tile([P, BLOCKS, N_MM], F32, name="soft", tag="soft3", align_bytes=64)
-        take_banks(3, 4)
-        for o in range(PASSES):
-            for c in range(BLOCKS):
-                multiply(3, c, o)
-        plain = BLOCKS - FUSED
-        soften(3, 4, plain)
-        for c in range(plain, BLOCKS):
-            soften_and_count(3, c)
-        count(0, 2, 1)
-        count(2, 4, 1)
-        count(0, 4, 2)
-        count(0, 2, 3)
-        store(0, 2)
-        if plain > 2:
-            count(2, plain, 3)
-        store(2, 4)
+        quantise(1, 2, 3)
+        quantise(1, 3, 4)
+        votes[0] = held.tile([P, 2, NQ // SEG], F32, name="votes", tag="votes0", align_bytes=64)
+        votes[1] = held.tile([P, 2, NQ // SEG], F32, name="votes", tag="votes1", align_bytes=64)
+        for n in range(PIECES):
+            if n in (1, 2):
+                take_banks(n, (2 * n + 2, 2 * n + 3))
+                by_block(n)
+            else:
+                take_banks(n, (0, 1, 2, 3))
+                by_pass(n)
+            soften(n, "soft%d" % n, 3 if n == PIECES - 1 else 4)
+        soften_and_count(3, 3)
+        for n in range(PIECES - 1):
+            count(n, 0, 2)
+            count(n, 2, 4)
+        count(3, 0, 2)
+        store(0)
+        count(3, 2, 3)
+        store(1)

@@ -30,7 +30,9 @@ ACT = mybir.ActivationFunctionType
 FLOPS = 2 * SLOTS * NQ * D
 BYTES = 4 * D * NQ + P * T * 4 + PASSES * 16 * T + 4 * T + 2 * P * SLOTS // 16 + 4 * SLOTS * NQ // SEG
 
-LATE_CUTS = ((0, 2), (2, 3), (3, 4))
+LOADS = ((0, 0, 4), (1, 0, 1), (1, 1, 2), (1, 2, 3), (1, 3, 4))
+AHEAD = 2
+GROUPS = (((0, 0),), ((1, 0),), ((2, 0), (3, 0)), ((0, 1),), ((1, 1),), ((2, 1),), ((3, 1),))
 
 def tile_attend_tok_votets_topk_kernel(tc, qT, k_words, k_scales, tt, offs, out):
     nc = tc.nc
@@ -46,16 +48,6 @@ def tile_attend_tok_votets_topk_kernel(tc, qT, k_words, k_scales, tt, offs, out)
         nc.sync.dma_start(offsets[:], offs)
         tt_pool = held.tile([P, T], F32, name="tt_pool", align_bytes=64)
         nc.scalar.dma_start(tt_pool[TT_ROW:P, :], tt[0:1, :])
-        raw = {}
-
-        def load_queries(o, n0, n1):
-            tile = held.tile([P, PACK, (n1 - n0) * N_MM], F32, name="raw", tag="raw%d%d" % (n0, o), align_bytes=64)
-            rows = qT[0, o * K_PASS : (o + 1) * K_PASS, n0 * N_MM : n1 * N_MM]
-            nc.sync.dma_start(tile[:], rows.rearrange("(p j) w -> p j w", j=PACK))
-            for n in range(n0, n1):
-                raw[n, o] = tile[:, :, (n - n0) * N_MM : (n - n0 + 1) * N_MM]
-
-        load_queries(0, 0, PIECES)
         word_pool = held.tile([P, T], U32, name="word_pool", align_bytes=64)
         nc.sync.dma_start(
             word_pool[:].bitcast(I32), k_words[0].rearrange("p t b -> p (t b)").bitcast(I32)
@@ -70,6 +62,18 @@ def tile_attend_tok_votets_topk_kernel(tc, qT, k_words, k_scales, tt, offs, out)
         nc.vector.memset(tt_pool[0:TT_ROW, :].bitcast(I32), 0)
         make_identity(nc, ident[:], nomemset=True)
 
+        raw = {}
+
+        def load_queries(o, n0, n1):
+            tile = held.tile([P, PACK, (n1 - n0) * N_MM], F32, name="raw", tag="raw%d%d" % (n0, o), align_bytes=64)
+            rows = qT[0, o * K_PASS : (o + 1) * K_PASS, n0 * N_MM : n1 * N_MM]
+            nc.sync.dma_start(tile[:], rows.rearrange("(p j) w -> p j w", j=PACK))
+            for n in range(n0, n1):
+                raw[n, o] = tile[:, :, (n - n0) * N_MM : (n - n0 + 1) * N_MM]
+
+        for load in LOADS[:AHEAD]:
+            load_queries(*load)
+
         picked_scales = held.tile([P, SLOTS], U8, name="picked_scales", align_bytes=64)
         nc.vector.tensor_copy(picked_scales[:], scale_pool[:].indirect(offsets[:]))
         key_scales = held.tile([P, PASSES, SLOTS], U8, name="key_scales", tag="scales", align_bytes=64)
@@ -78,21 +82,18 @@ def tile_attend_tok_votets_topk_kernel(tc, qT, k_words, k_scales, tt, offs, out)
                 key_scales[32 * quad : 32 * quad + 4].rearrange("p o n -> p (o n)").bitcast(I32),
                 picked_scales[LIVE + 8 * quad : LIVE + 8 * quad + 8, :].bitcast(I32),
             )
-        for n0, n1 in LATE_CUTS:
-            load_queries(1, n0, n1)
+        for load in LOADS[AHEAD:]:
+            load_queries(*load)
 
         picked_tt = held.tile([P, SLOTS], F32, name="picked_tt")
         nc.vector.tensor_copy(picked_tt[:], tt_pool[:].indirect(offsets[:]))
 
         picked_words = held.tile([P, SLOTS], U32, name="picked_words", align_bytes=64)
-
-        def gather_words(half):
-            s0 = half * HALF_LIST
+        for s0 in range(0, SLOTS, HALF_LIST):
             nc.vector.tensor_copy(
                 picked_words[:, s0 : s0 + HALF_LIST],
                 word_pool[:].indirect(offsets[:, s0 // 16 : (s0 + HALF_LIST) // 16]),
             )
-
         key_words = {}
 
         def part_words(half, tag):
@@ -107,33 +108,40 @@ def tile_attend_tok_votets_topk_kernel(tc, qT, k_words, k_scales, tt, offs, out)
         for c in range(BLOCKS):
             nc.tensor.transpose(turned[:, c, :], picked_tt[:, c * P : (c + 1) * P], ident[:])
 
-        q_codes = held.tile([P, PASSES, PIECES, N_MM], U32, name="q_codes", align_bytes=64)
-        q_scales = held.tile([P, PASSES, PIECES, N_MM], U8, name="q_scales", align_bytes=64)
-        grouped = held.tile([P, PASSES, PIECES, N_MM * PACK], BF16, name="grouped", align_bytes=64)
+        grouped, q_codes, q_scales, place = {}, {}, {}, {}
+        for g, units in enumerate(GROUPS):
+            grouped[g] = held.tile([P, len(units), K_PASS], BF16, name="grouped", tag="grouped%d" % g, align_bytes=64)
+            q_codes[g] = held.tile([P, len(units), N_MM], U32, name="q_codes", tag="codes%d" % g, align_bytes=64)
+            q_scales[g] = held.tile([P, len(units), N_MM], U8, name="q_scales", tag="q_scales%d" % g, align_bytes=64)
+            for u, unit in enumerate(units):
+                place[unit] = (g, u)
         on_scalar, on_vector = nc.scalar.copy, nc.vector.tensor_copy
         banks, soft, votes = {}, {}, {}
 
         def interleave(copy, n, o):
+            g, u = place[n, o]
             copy(
-                grouped[:, o, n, :].rearrange("p (c i t) -> p c t i", i=4, t=PACK),
+                grouped[g][:, u, :].rearrange("p (c i t) -> p c t i", i=4, t=PACK),
                 raw[n, o].rearrange("p t (c i) -> p c t i", i=4),
             )
 
-        def quantise(o, n0, n1):
+        def quantise(first, last):
+            (g, u0), u1 = place[first], place[last][1] + 1
             nc.vector.quantize_mx(
-                out=q_codes[:, o, n0:n1, :].rearrange("p n w -> p (n w)").bitcast(FP8X4),
-                scales=q_scales[:, o, n0:n1, :].rearrange("p n w -> p (n w)"),
-                in_=grouped[:, o, n0:n1, :].rearrange("p n w -> p (n w)"),
+                out=q_codes[g][:, u0:u1, :].rearrange("p u w -> p (u w)").bitcast(FP8X4),
+                scales=q_scales[g][:, u0:u1, :].rearrange("p u w -> p (u w)"),
+                in_=grouped[g][:, u0:u1, :].rearrange("p u w -> p (u w)"),
             )
 
         def multiply(n, c, o, first=0):
             half, s0 = divmod(c * P, HALF_LIST)
+            g, u = place[n, o]
             nc.tensor.matmul_mx(
                 out=banks[n, c],
                 lhsT=key_words[half][:, o, s0 : s0 + P].bitcast(FP4X4),
                 lhsT_scale=key_scales[:, o, c * P : (c + 1) * P],
-                rhs=q_codes[:, o, n, :].bitcast(FP8X4),
-                rhs_scale=q_scales[:, o, n, :],
+                rhs=q_codes[g][:, u, :].bitcast(FP8X4),
+                rhs_scale=q_scales[g][:, u, :],
                 start=(o == first),
                 stop=(o != first),
             )
@@ -185,41 +193,34 @@ def tile_attend_tok_votets_topk_kernel(tc, qT, k_words, k_scales, tt, offs, out)
             rows = out[0, 2 * pair * P : 2 * (pair + 1) * P, :]
             nc.sync.dma_start(rows.rearrange("(c p) j -> p c j", p=P), votes[pair][:])
 
-        bias = held.tile([P, BLOCKS], F32, name="bias", tag="bias", align_bytes=64)
-        nc.scalar.activation(bias[:], turned[:, :, TT_ROW], ACT.Copy, scale=-SHARP)
-        interleave(on_scalar, 0, 0)
-        interleave(on_vector, 3, 0)
-        interleave(on_scalar, 1, 0)
-        interleave(on_scalar, 2, 0)
-        quantise(0, 0, 2)
-        quantise(0, 2, 4)
-        gather_words(0)
-        gather_words(1)
         part_words(0, "words0")
         part_words(1, "words1")
-        interleave(on_scalar, 0, 1)
-        quantise(1, 0, 1)
-        interleave(on_scalar, 1, 1)
-        interleave(on_vector, 2, 1)
-        quantise(1, 1, 2)
-        interleave(on_vector, 3, 1)
-        quantise(1, 2, 3)
-        quantise(1, 3, 4)
+        bias = held.tile([P, BLOCKS], F32, name="bias", tag="bias", align_bytes=64)
+        nc.scalar.activation(bias[:], turned[:, :, TT_ROW], ACT.Copy, scale=-SHARP)
+        interleave(on_vector, 0, 0)
+        interleave(on_vector, 1, 0)
+        interleave(on_scalar, 2, 0)
+        interleave(on_scalar, 3, 0)
+        quantise((0, 0), (0, 0))
+        interleave(on_vector, 0, 1)
+        quantise((1, 0), (1, 0))
+        quantise((0, 1), (0, 1))
+        quantise((2, 0), (3, 0))
+        for n in range(1, PIECES):
+            interleave(on_vector, n, 1)
+            quantise((n, 1), (n, 1))
         votes[0] = held.tile([P, 2, NQ // SEG], F32, name="votes", tag="votes0", align_bytes=64)
         votes[1] = held.tile([P, 2, NQ // SEG], F32, name="votes", tag="votes1", align_bytes=64)
         for n in range(PIECES):
-            if n in (1, 2):
-                take_banks(n, (2 * n + 2, 2 * n + 3))
-                by_block(n)
-            else:
-                take_banks(n, (0, 1, 2, 3))
-                by_pass(n)
-            soften(n, "soft%d" % n, 3 if n == PIECES - 1 else 4)
+            take_banks(n, (4, 5, 6, 7) if n % 2 else (0, 1, 2, 3))
+            by_pass(n)
+            soften(n, "raw11" if n == 0 else "soft%d" % n, 3 if n == PIECES - 1 else 4)
         soften_and_count(3, 3)
         for n in range(PIECES - 1):
             count(n, 0, 2)
             count(n, 2, 4)
-        count(3, 0, 2)
+        count(3, 0, 1)
+        count(3, 1, 2)
         store(0)
         count(3, 2, 3)
         store(1)

@@ -13,7 +13,7 @@ N_MM = 128
 PIECES = NQ // N_MM
 RUNS = N_MM // SEG
 SHARP = 4.0
-LIVE = 96
+LIVE = 32
 TT_ROW = P - 1
 HALF_LIST = SLOTS // 2
 
@@ -30,7 +30,7 @@ ACT = mybir.ActivationFunctionType
 FLOPS = 2 * SLOTS * NQ * D
 BYTES = 4 * D * NQ + P * T * 4 + PASSES * 16 * T + 4 * T + 2 * P * SLOTS // 16 + 4 * SLOTS * NQ // SEG
 
-LOADS = ((0, 0, 4), (1, 0, 1), (1, 1, 2), (1, 2, 3), (1, 3, 4))
+LOADS = ((1, 0, 1), (0, 0, 4), (1, 1, 2), (1, 2, 3), (1, 3, 4))
 AHEAD = 2
 GROUPS = (((0, 0),), ((1, 0),), ((2, 0), (3, 0)), ((0, 1),), ((1, 1),), ((2, 1),), ((3, 1),))
 
@@ -42,7 +42,7 @@ def tile_attend_tok_votets_topk_kernel(tc, qT, k_words, k_scales, tt, offs, out)
 
         scale_pool = held.tile([P, T], U8, name="scale_pool", tag="scales", align_bytes=64)
         nc.sync.dma_start(
-            scale_pool[LIVE:P, :].bitcast(I32), k_scales.rearrange("o f t -> f o t").bitcast(I32)
+            scale_pool[LIVE : 2 * LIVE, :].bitcast(I32), k_scales.rearrange("o f t -> f o t").bitcast(I32)
         )
         offsets = held.tile([P, SLOTS // 16], U16, name="offsets")
         nc.sync.dma_start(offsets[:], offs)
@@ -56,7 +56,9 @@ def tile_attend_tok_votets_topk_kernel(tc, qT, k_words, k_scales, tt, offs, out)
         nc.gpsimd.memset(warm[:, 0:8], 0.0)
         nc.scalar.activation(warm[:, 8:16], warm[:, 0:8], ACT.Sigmoid)
         nc.vector.memset(scale_pool[0:LIVE, :].bitcast(I32), 0)
+        nc.vector.memset(scale_pool[2 * LIVE : P, :].bitcast(I32), 0)
 
+        key_scales = held.tile([P, PASSES, SLOTS], U8, name="key_scales", align_bytes=64)
         ident = held.tile([P, P], F32, name="ident")
         nc.vector.memset(ident[:], 0.0)
         nc.vector.memset(tt_pool[0:TT_ROW, :].bitcast(I32), 0)
@@ -74,9 +76,8 @@ def tile_attend_tok_votets_topk_kernel(tc, qT, k_words, k_scales, tt, offs, out)
         for load in LOADS[:AHEAD]:
             load_queries(*load)
 
-        picked_scales = held.tile([P, SLOTS], U8, name="picked_scales", align_bytes=64)
+        picked_scales = held.tile([P, SLOTS], U8, name="picked_scales", tag="picked_scales", align_bytes=64)
         nc.vector.tensor_copy(picked_scales[:], scale_pool[:].indirect(offsets[:]))
-        key_scales = held.tile([P, PASSES, SLOTS], U8, name="key_scales", tag="scales", align_bytes=64)
         for quad in (0, 2, 1, 3):
             nc.sync.dma_start(
                 key_scales[32 * quad : 32 * quad + 4].rearrange("p o n -> p (o n)").bitcast(I32),
@@ -110,11 +111,16 @@ def tile_attend_tok_votets_topk_kernel(tc, qT, k_words, k_scales, tt, offs, out)
 
         grouped, q_codes, q_scales, place = {}, {}, {}, {}
         for g, units in enumerate(GROUPS):
-            grouped[g] = held.tile([P, len(units), K_PASS], BF16, name="grouped", tag="grouped%d" % g, align_bytes=64)
+            if g != 2:
+                grouped[g] = held.tile([P, len(units), K_PASS], BF16, name="grouped", tag="grouped%d" % g, align_bytes=64)
             q_codes[g] = held.tile([P, len(units), N_MM], U32, name="q_codes", tag="codes%d" % g, align_bytes=64)
             q_scales[g] = held.tile([P, len(units), N_MM], U8, name="q_scales", tag="q_scales%d" % g, align_bytes=64)
             for u, unit in enumerate(units):
                 place[unit] = (g, u)
+
+        def late_group(g, tag):
+            grouped[g] = held.tile([P, 2, K_PASS], BF16, name="grouped", tag=tag, align_bytes=64)
+
         on_scalar, on_vector = nc.scalar.copy, nc.vector.tensor_copy
         banks, soft, votes = {}, {}, {}
 
@@ -194,29 +200,53 @@ def tile_attend_tok_votets_topk_kernel(tc, qT, k_words, k_scales, tt, offs, out)
             nc.sync.dma_start(rows.rearrange("(c p) j -> p c j", p=P), votes[pair][:])
 
         part_words(0, "words0")
-        part_words(1, "words1")
+        interleave(on_scalar, 0, 1)
         bias = held.tile([P, BLOCKS], F32, name="bias", tag="bias", align_bytes=64)
         nc.scalar.activation(bias[:], turned[:, :, TT_ROW], ACT.Copy, scale=-SHARP)
+        quantise((0, 1), (0, 1))
+        part_words(1, "raw01")
+        spare = psum.tile([P, PASSES * HALF_LIST], F32, name="spare", tag="bank7")
+        for turn in range(2):
+            nc.tensor.matmul_mx(
+                out=spare[:],
+                lhsT=q_codes[3][:, 0, :].bitcast(FP8X4),
+                lhsT_scale=q_scales[3][:, 0, :],
+                rhs=key_words[0][:].rearrange("p o n -> p (o n)").bitcast(FP4X4),
+                rhs_scale=scale_pool[:, 0:SLOTS],
+                start=True,
+                stop=True,
+            )
         interleave(on_vector, 0, 0)
         interleave(on_vector, 1, 0)
+        late_group(2, "picked_scales")
         interleave(on_scalar, 2, 0)
         interleave(on_scalar, 3, 0)
         quantise((0, 0), (0, 0))
-        interleave(on_vector, 0, 1)
         quantise((1, 0), (1, 0))
-        quantise((0, 1), (0, 1))
-        quantise((2, 0), (3, 0))
-        for n in range(1, PIECES):
-            interleave(on_vector, n, 1)
-            quantise((n, 1), (n, 1))
-        votes[0] = held.tile([P, 2, NQ // SEG], F32, name="votes", tag="votes0", align_bytes=64)
+        take_banks(0, (0, 1, 2, 3))
+        for o in (1, 0):
+            for c in range(BLOCKS):
+                multiply(0, c, o, first=1)
+        interleave(on_vector, 1, 1)
+        quantise((2, 0), (2, 0))
+        quantise((1, 1), (1, 1))
+        interleave(on_vector, 2, 1)
+        quantise((3, 0), (3, 0))
+        quantise((2, 1), (2, 1))
+        interleave(on_vector, 3, 1)
+        quantise((3, 1), (3, 1))
+        votes[0] = held.tile([P, 2, NQ // SEG], F32, name="votes", tag="grouped5", align_bytes=64)
         votes[1] = held.tile([P, 2, NQ // SEG], F32, name="votes", tag="votes1", align_bytes=64)
-        for n in range(PIECES):
+        soften(0, "soft0", 3)
+        soften_and_count(0, 3)
+        for n in range(1, PIECES):
             take_banks(n, (4, 5, 6, 7) if n % 2 else (0, 1, 2, 3))
             by_pass(n)
-            soften(n, "raw11" if n == 0 else "soft%d" % n, 3 if n == PIECES - 1 else 4)
+            soften(n, "soft%d" % n, 3 if n == PIECES - 1 else 4)
         soften_and_count(3, 3)
-        for n in range(PIECES - 1):
+        count(0, 0, 2)
+        count(0, 2, 3)
+        for n in (1, 2):
             count(n, 0, 2)
             count(n, 2, 4)
         count(3, 0, 1)

@@ -13,7 +13,7 @@ N_MM = 128
 PIECES = NQ // N_MM
 RUNS = N_MM // SEG
 SHARP = 4.0
-LIVE = 32
+LIVE = 96
 TT_ROW = P - 1
 HALF_LIST = SLOTS // 2
 
@@ -42,7 +42,7 @@ def tile_attend_tok_votets_topk_kernel(tc, qT, k_words, k_scales, tt, offs, out)
 
         scale_pool = held.tile([P, T], U8, name="scale_pool", tag="scales", align_bytes=64)
         nc.sync.dma_start(
-            scale_pool[LIVE : 2 * LIVE, :].bitcast(I32), k_scales.rearrange("o f t -> f o t").bitcast(I32)
+            scale_pool[LIVE:P, :].bitcast(I32), k_scales.rearrange("o f t -> f o t").bitcast(I32)
         )
         offsets = held.tile([P, SLOTS // 16], U16, name="offsets")
         nc.sync.dma_start(offsets[:], offs)
@@ -52,11 +52,10 @@ def tile_attend_tok_votets_topk_kernel(tc, qT, k_words, k_scales, tt, offs, out)
         nc.sync.dma_start(
             word_pool[:].bitcast(I32), k_words[0].rearrange("p t b -> p (t b)").bitcast(I32)
         )
-        warm = held.tile([P, 16], F32, name="warm")
+        warm = held.tile([P, 16], F32, name="warm", tag="picked_scales", align_bytes=64)
         nc.gpsimd.memset(warm[:, 0:8], 0.0)
         nc.scalar.activation(warm[:, 8:16], warm[:, 0:8], ACT.Sigmoid)
         nc.vector.memset(scale_pool[0:LIVE, :].bitcast(I32), 0)
-        nc.vector.memset(scale_pool[2 * LIVE : P, :].bitcast(I32), 0)
 
         key_scales = held.tile([P, PASSES, SLOTS], U8, name="key_scales", align_bytes=64)
         ident = held.tile([P, P], F32, name="ident")
@@ -78,16 +77,20 @@ def tile_attend_tok_votets_topk_kernel(tc, qT, k_words, k_scales, tt, offs, out)
 
         picked_scales = held.tile([P, SLOTS], U8, name="picked_scales", tag="picked_scales", align_bytes=64)
         nc.vector.tensor_copy(picked_scales[:], scale_pool[:].indirect(offsets[:]))
+        picked_tt = held.tile([P, SLOTS], F32, name="picked_tt", tag="picked_tt", align_bytes=64)
+        nc.vector.tensor_copy(picked_tt[:], tt_pool[:].indirect(offsets[:]))
+        dealt = held.tile([P, SLOTS], U8, name="dealt", tag="dealt", align_bytes=64)
+        nc.vector.tensor_copy(
+            dealt[:].rearrange("p (h c q) -> p h q c", h=2, c=2),
+            picked_scales[:].rearrange("p (h q c) -> p h q c", h=2, c=2),
+        )
         for quad in (0, 2, 1, 3):
             nc.sync.dma_start(
                 key_scales[32 * quad : 32 * quad + 4].rearrange("p o n -> p (o n)").bitcast(I32),
-                picked_scales[LIVE + 8 * quad : LIVE + 8 * quad + 8, :].bitcast(I32),
+                dealt[LIVE + 8 * quad : LIVE + 8 * quad + 8, :].bitcast(I32),
             )
         for load in LOADS[AHEAD:]:
             load_queries(*load)
-
-        picked_tt = held.tile([P, SLOTS], F32, name="picked_tt")
-        nc.vector.tensor_copy(picked_tt[:], tt_pool[:].indirect(offsets[:]))
 
         picked_words = held.tile([P, SLOTS], U32, name="picked_words", align_bytes=64)
         for s0 in range(0, SLOTS, HALF_LIST):
@@ -101,13 +104,13 @@ def tile_attend_tok_votets_topk_kernel(tc, qT, k_words, k_scales, tt, offs, out)
             s0 = half * HALF_LIST
             key_words[half] = held.tile([P, PASSES, HALF_LIST], U16, name="key_words", tag=tag, align_bytes=64)
             nc.vector.tensor_copy(
-                key_words[half][:],
-                picked_words[:, s0 : s0 + HALF_LIST].bitcast(U16).rearrange("p (n o) -> p o n", o=PASSES),
+                key_words[half][:].rearrange("p o (c q) -> p o q c", c=2),
+                picked_words[:, s0 : s0 + HALF_LIST].bitcast(U16).rearrange("p (q c o) -> p o q c", c=2, o=PASSES),
             )
 
         turned = psum.tile([P, BLOCKS, P], F32, name="turned", tag="bank7")
         for c in range(BLOCKS):
-            nc.tensor.transpose(turned[:, c, :], picked_tt[:, c * P : (c + 1) * P], ident[:])
+            nc.tensor.transpose(turned[:, c, :], picked_tt[:, c // 2 * HALF_LIST + c % 2 : (c // 2 + 1) * HALF_LIST : 2], ident[:])
 
         grouped, q_codes, q_scales, place = {}, {}, {}, {}
         for g, units in enumerate(GROUPS):
@@ -197,7 +200,7 @@ def tile_attend_tok_votets_topk_kernel(tc, qT, k_words, k_scales, tt, offs, out)
 
         def store(pair):
             rows = out[0, 2 * pair * P : 2 * (pair + 1) * P, :]
-            nc.sync.dma_start(rows.rearrange("(c p) j -> p c j", p=P), votes[pair][:])
+            nc.sync.dma_start(rows.rearrange("(p c) j -> p c j", c=2), votes[pair][:])
 
         part_words(0, "words0")
         interleave(on_scalar, 0, 1)
@@ -218,7 +221,7 @@ def tile_attend_tok_votets_topk_kernel(tc, qT, k_words, k_scales, tt, offs, out)
             )
         interleave(on_vector, 0, 0)
         interleave(on_vector, 1, 0)
-        late_group(2, "picked_scales")
+        late_group(2, "dealt")
         interleave(on_scalar, 2, 0)
         interleave(on_scalar, 3, 0)
         quantise((0, 0), (0, 0))

@@ -16,6 +16,12 @@ SHARP = 4.0
 LIVE = 96
 TT_ROW = P - 1
 HALF_LIST = SLOTS // 2
+WARM_PASSES = 2
+
+LOADS = ((1, 0, 1), (0, 0, PIECES), (1, 1, 2), (1, 2, 3), (1, 3, 4))
+AHEAD = 2
+GROUPS = (((0, 0),), ((1, 0),), ((2, 0), (3, 0)), ((0, 1),), ((1, 1),), ((2, 1),), ((3, 1),))
+SCALAR_PAIR = 2
 
 F32 = mybir.dt.float32
 BF16 = mybir.dt.bfloat16
@@ -30,9 +36,6 @@ ACT = mybir.ActivationFunctionType
 FLOPS = 2 * SLOTS * NQ * D
 BYTES = 4 * D * NQ + P * T * 4 + PASSES * 16 * T + 4 * T + 2 * P * SLOTS // 16 + 4 * SLOTS * NQ // SEG
 
-LOADS = ((1, 0, 1), (0, 0, 4), (1, 1, 2), (1, 2, 3), (1, 3, 4))
-AHEAD = 2
-GROUPS = (((0, 0),), ((1, 0),), ((2, 0), (3, 0)), ((0, 1),), ((1, 1),), ((2, 1),), ((3, 1),))
 
 def tile_attend_tok_votets_topk_kernel(tc, qT, k_words, k_scales, tt, offs, out):
     nc = tc.nc
@@ -66,7 +69,9 @@ def tile_attend_tok_votets_topk_kernel(tc, qT, k_words, k_scales, tt, offs, out)
         raw = {}
 
         def load_queries(o, n0, n1):
-            tile = held.tile([P, PACK, (n1 - n0) * N_MM], F32, name="raw", tag="raw%d%d" % (n0, o), align_bytes=64)
+            tile = held.tile(
+                [P, PACK, (n1 - n0) * N_MM], F32, name="raw", tag="raw%d%d" % (n0, o), align_bytes=64
+            )
             rows = qT[0, o * K_PASS : (o + 1) * K_PASS, n0 * N_MM : n1 * N_MM]
             nc.sync.dma_start(tile[:], rows.rearrange("(p j) w -> p j w", j=PACK))
             for n in range(n0, n1):
@@ -100,29 +105,35 @@ def tile_attend_tok_votets_topk_kernel(tc, qT, k_words, k_scales, tt, offs, out)
             )
         key_words = {}
 
-        def part_words(half, tag):
+        def part_words(half):
             s0 = half * HALF_LIST
-            key_words[half] = held.tile([P, PASSES, HALF_LIST], U16, name="key_words", tag=tag, align_bytes=64)
+            key_words[half] = parted[:, half]
             nc.vector.tensor_copy(
-                key_words[half][:].rearrange("p o (c q) -> p o q c", c=2),
-                picked_words[:, s0 : s0 + HALF_LIST].bitcast(U16).rearrange("p (q c o) -> p o q c", c=2, o=PASSES),
+                key_words[half].rearrange("p o (c q) -> p o q c", c=2),
+                picked_words[:, s0 : s0 + HALF_LIST]
+                .bitcast(U16)
+                .rearrange("p (q c o) -> p o q c", c=2, o=PASSES),
             )
 
         turned = psum.tile([P, BLOCKS, P], F32, name="turned", tag="bank7")
         for c in range(BLOCKS):
-            nc.tensor.transpose(turned[:, c, :], picked_tt[:, c // 2 * HALF_LIST + c % 2 : (c // 2 + 1) * HALF_LIST : 2], ident[:])
+            half = c // 2
+            nc.tensor.transpose(
+                turned[:, c, :], picked_tt[:, half * HALF_LIST + c % 2 : (half + 1) * HALF_LIST : 2], ident[:]
+            )
 
         grouped, q_codes, q_scales, place = {}, {}, {}, {}
         for g, units in enumerate(GROUPS):
-            if g != 2:
-                grouped[g] = held.tile([P, len(units), K_PASS], BF16, name="grouped", tag="grouped%d" % g, align_bytes=64)
+            if g != SCALAR_PAIR:
+                grouped[g] = held.tile(
+                    [P, len(units), K_PASS], BF16, name="grouped", tag="grouped%d" % g, align_bytes=64
+                )
             q_codes[g] = held.tile([P, len(units), N_MM], U32, name="q_codes", tag="codes%d" % g, align_bytes=64)
-            q_scales[g] = held.tile([P, len(units), N_MM], U8, name="q_scales", tag="q_scales%d" % g, align_bytes=64)
+            q_scales[g] = held.tile(
+                [P, len(units), N_MM], U8, name="q_scales", tag="q_scales%d" % g, align_bytes=64
+            )
             for u, unit in enumerate(units):
                 place[unit] = (g, u)
-
-        def late_group(g, tag):
-            grouped[g] = held.tile([P, 2, K_PASS], BF16, name="grouped", tag=tag, align_bytes=64)
 
         on_scalar, on_vector = nc.scalar.copy, nc.vector.tensor_copy
         banks, soft, votes = {}, {}, {}
@@ -134,25 +145,10 @@ def tile_attend_tok_votets_topk_kernel(tc, qT, k_words, k_scales, tt, offs, out)
                 raw[n, o].rearrange("p t (c i) -> p c t i", i=4),
             )
 
-        def quantise(first, last):
-            (g, u0), u1 = place[first], place[last][1] + 1
-            nc.vector.quantize_mx(
-                out=q_codes[g][:, u0:u1, :].rearrange("p u w -> p (u w)").bitcast(FP8X4),
-                scales=q_scales[g][:, u0:u1, :].rearrange("p u w -> p (u w)"),
-                in_=grouped[g][:, u0:u1, :].rearrange("p u w -> p (u w)"),
-            )
-
-        def multiply(n, c, o, first=0):
-            half, s0 = divmod(c * P, HALF_LIST)
+        def quantise(n, o):
             g, u = place[n, o]
-            nc.tensor.matmul_mx(
-                out=banks[n, c],
-                lhsT=key_words[half][:, o, s0 : s0 + P].bitcast(FP4X4),
-                lhsT_scale=key_scales[:, o, c * P : (c + 1) * P],
-                rhs=q_codes[g][:, u, :].bitcast(FP8X4),
-                rhs_scale=q_scales[g][:, u, :],
-                start=(o == first),
-                stop=(o != first),
+            nc.vector.quantize_mx(
+                out=q_codes[g][:, u, :].bitcast(FP8X4), scales=q_scales[g][:, u, :], in_=grouped[g][:, u, :]
             )
 
         def take_banks(n, numbers):
@@ -162,18 +158,23 @@ def tile_attend_tok_votets_topk_kernel(tc, qT, k_words, k_scales, tt, offs, out)
                 for c in range(shared):
                     banks[n, i * shared + c] = bank[:, c, :]
 
-        def by_block(n):
-            for c in range(BLOCKS):
-                for o in range(PASSES):
-                    multiply(n, c, o)
+        def multiply(n, blocks, passes):
+            for o in passes:
+                g, u = place[n, o]
+                for c in blocks:
+                    half, s0 = divmod(c * P, HALF_LIST)
+                    nc.tensor.matmul_mx(
+                        out=banks[n, c],
+                        lhsT=key_words[half][:, o, s0 : s0 + P].bitcast(FP4X4),
+                        lhsT_scale=key_scales[:, o, c * P : (c + 1) * P],
+                        rhs=q_codes[g][:, u, :].bitcast(FP8X4),
+                        rhs_scale=q_scales[g][:, u, :],
+                        start=(o == passes[0]),
+                        stop=(o == passes[-1]),
+                    )
 
-        def by_pass(n):
-            for o in range(PASSES):
-                for c in range(BLOCKS):
-                    multiply(n, c, o)
-
-        def soften(n, tag, blocks=BLOCKS):
-            soft[n] = held.tile([P, BLOCKS, N_MM], F32, name="soft", tag=tag, align_bytes=64)
+        def soften(n, blocks):
+            soft[n] = held.tile([P, BLOCKS, N_MM], F32, name="soft", tag="soft%d" % n, align_bytes=64)
             for c in range(blocks):
                 nc.scalar.activation(
                     soft[n][:, c, :], banks[n, c], ACT.Sigmoid, bias=bias[:, c : c + 1], scale=SHARP
@@ -198,62 +199,71 @@ def tile_attend_tok_votets_topk_kernel(tc, qT, k_words, k_scales, tt, offs, out)
                 mybir.AluOpType.add,
             )
 
-        def store(pair):
-            rows = out[0, 2 * pair * P : 2 * (pair + 1) * P, :]
-            nc.sync.dma_start(rows.rearrange("(p c) j -> p c j", c=2), votes[pair][:])
+        def store(half):
+            rows = out[0, half * HALF_LIST : (half + 1) * HALF_LIST, :]
+            nc.sync.dma_start(rows.rearrange("(p c) j -> p c j", c=2), votes[half][:])
 
-        part_words(0, "words0")
         interleave(on_scalar, 0, 1)
         bias = held.tile([P, BLOCKS], F32, name="bias", tag="bias", align_bytes=64)
         nc.scalar.activation(bias[:], turned[:, :, TT_ROW], ACT.Copy, scale=-SHARP)
-        quantise((0, 1), (0, 1))
-        part_words(1, "raw01")
+        quantise(0, 1)
+        parted = held.tile([P, 2, PASSES, HALF_LIST], U16, name="parted", tag="raw01", align_bytes=64)
+        part_words(0)
+        part_words(1)
+        early = place[0, 1][0]
         spare = psum.tile([P, PASSES * HALF_LIST], F32, name="spare", tag="bank7")
-        for turn in range(2):
+        for _ in range(WARM_PASSES):
             nc.tensor.matmul_mx(
                 out=spare[:],
-                lhsT=q_codes[3][:, 0, :].bitcast(FP8X4),
-                lhsT_scale=q_scales[3][:, 0, :],
-                rhs=key_words[0][:].rearrange("p o n -> p (o n)").bitcast(FP4X4),
+                lhsT=q_codes[early][:, 0, :].bitcast(FP8X4),
+                lhsT_scale=q_scales[early][:, 0, :],
+                rhs=picked_words[:, 0:HALF_LIST].bitcast(FP4X4),
                 rhs_scale=scale_pool[:, 0:SLOTS],
                 start=True,
                 stop=True,
             )
+
         interleave(on_vector, 0, 0)
         interleave(on_vector, 1, 0)
-        late_group(2, "dealt")
+        grouped[SCALAR_PAIR] = held.tile([P, 2, K_PASS], BF16, name="grouped", tag="dealt", align_bytes=64)
         interleave(on_scalar, 2, 0)
         interleave(on_scalar, 3, 0)
-        quantise((0, 0), (0, 0))
-        quantise((1, 0), (1, 0))
+        quantise(0, 0)
+        quantise(1, 0)
         take_banks(0, (0, 1, 2, 3))
-        for o in (1, 0):
-            for c in range(BLOCKS):
-                multiply(0, c, o, first=1)
-        interleave(on_vector, 1, 1)
-        quantise((2, 0), (2, 0))
-        quantise((1, 1), (1, 1))
-        interleave(on_vector, 2, 1)
-        quantise((3, 0), (3, 0))
-        quantise((2, 1), (2, 1))
-        interleave(on_vector, 3, 1)
-        quantise((3, 1), (3, 1))
-        votes[0] = held.tile([P, 2, NQ // SEG], F32, name="votes", tag="grouped5", align_bytes=64)
-        votes[1] = held.tile([P, 2, NQ // SEG], F32, name="votes", tag="votes1", align_bytes=64)
-        soften(0, "soft0", 3)
-        soften_and_count(0, 3)
+        multiply(0, range(BLOCKS), (1, 0))
+
         for n in range(1, PIECES):
-            take_banks(n, (4, 5, 6, 7) if n % 2 else (0, 1, 2, 3))
-            by_pass(n)
-            soften(n, "soft%d" % n, 3 if n == PIECES - 1 else 4)
-        soften_and_count(3, 3)
-        count(0, 0, 2)
-        count(0, 2, 3)
-        for n in (1, 2):
+            interleave(on_vector, n, 1)
+            if n + 1 < PIECES:
+                quantise(n + 1, 0)
+            quantise(n, 1)
+
+        votes[0] = held.tile(
+            [P, 2, NQ // SEG], F32, name="votes", tag="grouped%d" % place[2, 1][0], align_bytes=64
+        )
+        votes[1] = held.tile([P, 2, NQ // SEG], F32, name="votes", tag="votes1", align_bytes=64)
+
+        last = PIECES - 1
+        soften(0, BLOCKS - 1)
+        soften_and_count(0, BLOCKS - 1)
+        take_banks(1, (4, 5))
+        for c in range(BLOCKS):
+            multiply(1, (c,), (0, 1))
+        soften(1, BLOCKS)
+        take_banks(2, (0, 1, 2, 3))
+        multiply(2, range(BLOCKS), (0, 1))
+        soften(2, BLOCKS)
+        take_banks(last, (6, 7, 4, 5))
+        multiply(last, range(BLOCKS - 1), (0, 1))
+        multiply(last, (BLOCKS - 1,), (0, 1))
+        soften(last, BLOCKS - 1)
+        soften_and_count(last, BLOCKS - 1)
+        for n in range(last):
             count(n, 0, 2)
-            count(n, 2, 4)
-        count(3, 0, 1)
-        count(3, 1, 2)
+            count(n, 2, BLOCKS - 1 if n == 0 else BLOCKS)
+        count(last, 0, 1)
+        count(last, 1, 2)
         store(0)
-        count(3, 2, 3)
+        count(last, 2, 3)
         store(1)

@@ -9,19 +9,12 @@ K_PASS = P * PACK
 D, T, SLOTS, NQ, SEG = 1024, 2048, 512, 512, 32
 PASSES = D // K_PASS
 BLOCKS = SLOTS // P
-N_MM = 128
-PIECES = NQ // N_MM
-RUNS = N_MM // SEG
+PIECE = 128
+RUNS = PIECE // SEG
 SHARP = 4.0
 LIVE = 96
 TT_ROW = P - 1
 HALF_LIST = SLOTS // 2
-WARM_PASSES = 2
-
-LOADS = ((1, 0, 1), (0, 0, PIECES), (1, 1, 2), (1, 2, 3), (1, 3, 4))
-AHEAD = 2
-GROUPS = (((0, 0),), ((1, 0),), ((2, 0), (3, 0)), ((0, 1),), ((1, 1),), ((2, 1),), ((3, 1),))
-SCALAR_PAIR = 2
 
 F32 = mybir.dt.float32
 BF16 = mybir.dt.bfloat16
@@ -43,7 +36,7 @@ def tile_attend_tok_votets_topk_kernel(tc, qT, k_words, k_scales, tt, offs, out)
         held = ctx.enter_context(tc.tile_pool(name="held", bufs=1))
         psum = ctx.enter_context(tc.psum_pool(name="psum", bufs=1))
 
-        scale_pool = held.tile([P, T], U8, name="scale_pool", tag="scales", align_bytes=64)
+        scale_pool = held.tile([P, T], U8, name="scale_pool", align_bytes=64)
         nc.sync.dma_start(
             scale_pool[LIVE:P, :].bitcast(I32), k_scales.rearrange("o f t -> f o t").bitcast(I32)
         )
@@ -55,47 +48,54 @@ def tile_attend_tok_votets_topk_kernel(tc, qT, k_words, k_scales, tt, offs, out)
         nc.sync.dma_start(
             word_pool[:].bitcast(I32), k_words[0].rearrange("p t b -> p (t b)").bitcast(I32)
         )
-        warm = held.tile([P, 16], F32, name="warm", tag="picked_scales", align_bytes=64)
+        warm = held.tile([P, 16], F32, name="warm", align_bytes=64)
         nc.gpsimd.memset(warm[:, 0:8], 0.0)
         nc.scalar.activation(warm[:, 8:16], warm[:, 0:8], ACT.Sigmoid)
         nc.vector.memset(scale_pool[0:LIVE, :].bitcast(I32), 0)
-
-        key_scales = held.tile([P, PASSES, SLOTS], U8, name="key_scales", align_bytes=64)
-        ident = held.tile([P, P], F32, name="ident")
-        nc.vector.memset(ident[:], 0.0)
         nc.vector.memset(tt_pool[0:TT_ROW, :].bitcast(I32), 0)
-        make_identity(nc, ident[:], nomemset=True)
+        ident = held.tile([P, P], F32, name="ident")
+        make_identity(nc, ident[:])
 
         raw = {}
 
-        def load_queries(o, n0, n1):
-            tile = held.tile(
-                [P, PACK, (n1 - n0) * N_MM], F32, name="raw", tag="raw%d%d" % (n0, o), align_bytes=64
-            )
-            rows = qT[0, o * K_PASS : (o + 1) * K_PASS, n0 * N_MM : n1 * N_MM]
-            nc.sync.dma_start(tile[:], rows.rearrange("(p j) w -> p j w", j=PACK))
+        raw_tiles = {}
+
+        def load_queries(o, n0, n1, t0=0, t1=PACK):
+            if t0 == 0:
+                raw_tiles[n0, o] = held.tile(
+                    [P, PACK, (n1 - n0) * PIECE], F32, name="raw", tag="raw%d%d" % (n0, o), align_bytes=64
+                )
+            tile = raw_tiles[n0, o]
+            rows = qT[0, o * K_PASS : (o + 1) * K_PASS, n0 * PIECE : n1 * PIECE]
+            nc.sync.dma_start(tile[:, t0:t1, :], rows.rearrange("(p j) w -> p j w", j=PACK)[:, t0:t1, :])
             for n in range(n0, n1):
-                raw[n, o] = tile[:, :, (n - n0) * N_MM : (n - n0 + 1) * N_MM]
+                raw[n, o] = tile[:, :, (n - n0) * PIECE : (n - n0 + 1) * PIECE]
 
-        for load in LOADS[:AHEAD]:
-            load_queries(*load)
+        load_queries(1, 0, 2)
+        load_queries(0, 0, 2, 0, 2)
 
-        picked_scales = held.tile([P, SLOTS], U8, name="picked_scales", tag="picked_scales", align_bytes=64)
-        nc.vector.tensor_copy(picked_scales[:], scale_pool[:].indirect(offsets[:]))
-        picked_tt = held.tile([P, SLOTS], F32, name="picked_tt", tag="picked_tt", align_bytes=64)
-        nc.vector.tensor_copy(picked_tt[:], tt_pool[:].indirect(offsets[:]))
-        dealt = held.tile([P, SLOTS], U8, name="dealt", tag="dealt", align_bytes=64)
+        picked_scales = held.tile([P, SLOTS], U8, name="picked_scales", align_bytes=64)
         nc.vector.tensor_copy(
-            dealt[:].rearrange("p (h c q) -> p h q c", h=2, c=2),
-            picked_scales[:].rearrange("p (h q c) -> p h q c", h=2, c=2),
+            picked_scales[:].rearrange("p (c q) -> p q c", c=BLOCKS), scale_pool[:].indirect(offsets[:])
         )
+        key_scales = held.tile([P, PASSES, SLOTS], U8, name="key_scales", align_bytes=64)
         for quad in (0, 2, 1, 3):
             nc.sync.dma_start(
                 key_scales[32 * quad : 32 * quad + 4].rearrange("p o n -> p (o n)").bitcast(I32),
-                dealt[LIVE + 8 * quad : LIVE + 8 * quad + 8, :].bitcast(I32),
+                picked_scales[LIVE + 8 * quad : LIVE + 8 * quad + 8, :].bitcast(I32),
             )
-        for load in LOADS[AHEAD:]:
-            load_queries(*load)
+        load_queries(0, 0, 2, 2, PACK)
+        load_queries(0, 2, 4)
+        load_queries(1, 2, 3)
+        load_queries(1, 3, 4)
+
+        picked_tt = held.tile([P, SLOTS], F32, name="picked_tt", align_bytes=64)
+        nc.scalar.activation(picked_tt[:], tt_pool[:].indirect(offsets[:]), ACT.Copy)
+        turned = psum.tile([P, BLOCKS, P], F32, name="turned", tag="bank7")
+        for c in range(BLOCKS):
+            nc.tensor.transpose(turned[:, c, :], picked_tt[:, c:SLOTS:BLOCKS], ident[:])
+        bias = held.tile([P, BLOCKS], F32, name="bias", align_bytes=64)
+        nc.scalar.activation(bias[:], turned[:, :, TT_ROW], ACT.Copy, scale=-SHARP)
 
         picked_words = held.tile([P, SLOTS], U32, name="picked_words", align_bytes=64)
         for s0 in range(0, SLOTS, HALF_LIST):
@@ -103,81 +103,73 @@ def tile_attend_tok_votets_topk_kernel(tc, qT, k_words, k_scales, tt, offs, out)
                 picked_words[:, s0 : s0 + HALF_LIST],
                 word_pool[:].indirect(offsets[:, s0 // 16 : (s0 + HALF_LIST) // 16]),
             )
-        key_words = {}
+        key_words = held.tile([P, PASSES, SLOTS], U16, name="key_words", align_bytes=64)
 
-        def part_words(half):
-            s0 = half * HALF_LIST
-            key_words[half] = parted[:, half]
+        def part_words(o, s0, s1):
             nc.vector.tensor_copy(
-                key_words[half].rearrange("p o (c q) -> p o q c", c=2),
-                picked_words[:, s0 : s0 + HALF_LIST]
-                .bitcast(U16)
-                .rearrange("p (q c o) -> p o q c", c=2, o=PASSES),
+                key_words[:, o, :].rearrange("p (c q) -> p q c", c=BLOCKS)[:, s0 // BLOCKS : s1 // BLOCKS, :],
+                picked_words[:, s0:s1].bitcast(U16).rearrange("p (q c o) -> p o q c", c=BLOCKS, o=PASSES)[:, o],
             )
 
-        turned = psum.tile([P, BLOCKS, P], F32, name="turned", tag="bank7")
-        for c in range(BLOCKS):
-            half = c // 2
-            nc.tensor.transpose(
-                turned[:, c, :], picked_tt[:, half * HALF_LIST + c % 2 : (half + 1) * HALF_LIST : 2], ident[:]
-            )
-
-        grouped, q_codes, q_scales, place = {}, {}, {}, {}
-        for g, units in enumerate(GROUPS):
-            if g != SCALAR_PAIR:
-                grouped[g] = held.tile(
-                    [P, len(units), K_PASS], BF16, name="grouped", tag="grouped%d" % g, align_bytes=64
+        grouped, q_codes, q_scales = {}, {}, {}
+        for o in range(PASSES):
+            for half in range(2):
+                q_codes[half, o] = held.tile(
+                    [P, 2 * PIECE], U32, name="q_codes", tag="codes%d%d" % (half, o), align_bytes=64
                 )
-            q_codes[g] = held.tile([P, len(units), N_MM], U32, name="q_codes", tag="codes%d" % g, align_bytes=64)
-            q_scales[g] = held.tile(
-                [P, len(units), N_MM], U8, name="q_scales", tag="q_scales%d" % g, align_bytes=64
-            )
-            for u, unit in enumerate(units):
-                place[unit] = (g, u)
-
+                q_scales[half, o] = held.tile(
+                    [P, 2 * PIECE], U8, name="q_scales", tag="q_scales%d%d" % (half, o), align_bytes=64
+                )
         on_scalar, on_vector = nc.scalar.copy, nc.vector.tensor_copy
-        banks, soft, votes = {}, {}, {}
 
-        def interleave(copy, n, o):
-            g, u = place[n, o]
+        def interleave(copy, n, o, tag=None):
+            grouped[n, o] = held.tile(
+                [P, K_PASS], BF16, name="grouped", tag=tag or "grouped%d%d" % (n, o), align_bytes=64
+            )
             copy(
-                grouped[g][:, u, :].rearrange("p (c i t) -> p c t i", i=4, t=PACK),
+                grouped[n, o][:].rearrange("p (c i t) -> p c t i", i=4, t=PACK),
                 raw[n, o].rearrange("p t (c i) -> p c t i", i=4),
             )
 
         def quantise(n, o):
-            g, u = place[n, o]
+            cols = slice(n % 2 * PIECE, (n % 2 + 1) * PIECE)
             nc.vector.quantize_mx(
-                out=q_codes[g][:, u, :].bitcast(FP8X4), scales=q_scales[g][:, u, :], in_=grouped[g][:, u, :]
+                out=q_codes[n // 2, o][:, cols].bitcast(FP8X4),
+                scales=q_scales[n // 2, o][:, cols],
+                in_=grouped[n, o][:],
             )
 
-        def take_banks(n, numbers):
-            shared = BLOCKS // len(numbers)
-            for i, number in enumerate(numbers):
-                bank = psum.tile([P, shared, N_MM], F32, name="acc", tag="bank%d" % number)
-                for c in range(shared):
-                    banks[n, i * shared + c] = bank[:, c, :]
+        banks, soft = {}, {}
 
-        def multiply(n, blocks, passes):
-            for o in passes:
-                g, u = place[n, o]
-                for c in blocks:
-                    half, s0 = divmod(c * P, HALF_LIST)
-                    nc.tensor.matmul_mx(
-                        out=banks[n, c],
-                        lhsT=key_words[half][:, o, s0 : s0 + P].bitcast(FP4X4),
-                        lhsT_scale=key_scales[:, o, c * P : (c + 1) * P],
-                        rhs=q_codes[g][:, u, :].bitcast(FP8X4),
-                        rhs_scale=q_scales[g][:, u, :],
-                        start=(o == passes[0]),
-                        stop=(o == passes[-1]),
-                    )
+        def take_banks(n0, n1, first_bank):
+            for c in range(BLOCKS):
+                bank = psum.tile([P, (n1 - n0) * PIECE], F32, name="acc", tag="bank%d" % (first_bank + c))
+                banks[n0, c] = bank[:]
 
-        def soften(n, blocks):
-            soft[n] = held.tile([P, BLOCKS, N_MM], F32, name="soft", tag="soft%d" % n, align_bytes=64)
-            for c in range(blocks):
+        def multiply(group, n0, n1, o, start, stop):
+            cols = slice(n0 % 2 * PIECE, n0 % 2 * PIECE + (n1 - n0) * PIECE)
+            for c in range(BLOCKS):
+                nc.tensor.matmul_mx(
+                    out=banks[group, c][:, (n0 - group) * PIECE : (n1 - group) * PIECE],
+                    lhsT=key_words[:, o, c * P : (c + 1) * P].bitcast(FP4X4),
+                    lhsT_scale=key_scales[:, o, c * P : (c + 1) * P],
+                    rhs=q_codes[n0 // 2, o][:, cols].bitcast(FP8X4),
+                    rhs_scale=q_scales[n0 // 2, o][:, cols],
+                    start=start,
+                    stop=stop,
+                )
+
+        votes = [
+            held.tile([P, 2, NQ // SEG], F32, name="votes", tag="votes%d" % h, align_bytes=64) for h in range(2)
+        ]
+
+        def take_soft(n0, n1, tag):
+            soft[n0] = held.tile([P, BLOCKS, (n1 - n0) * PIECE], F32, name="soft", tag=tag, align_bytes=64)
+
+        def soften(n0, blocks):
+            for c in blocks:
                 nc.scalar.activation(
-                    soft[n][:, c, :], banks[n, c], ACT.Sigmoid, bias=bias[:, c : c + 1], scale=SHARP
+                    soft[n0][:, c, :], banks[n0, c], ACT.Sigmoid, bias=bias[:, c : c + 1], scale=SHARP
                 )
 
         def soften_and_count(n, c):
@@ -191,79 +183,60 @@ def tile_attend_tok_votets_topk_kernel(tc, qT, k_words, k_scales, tt, offs, out)
                     accum_out=votes[c // 2][:, c % 2, n * RUNS + j : n * RUNS + j + 1],
                 )
 
-        def count(n, c0, c1):
+        def count(n0, n1, c0, c1):
             nc.vector.tensor_reduce(
-                votes[c0 // 2][:, c0 % 2 : c0 % 2 + c1 - c0, n * RUNS : (n + 1) * RUNS],
-                soft[n][:, c0:c1, :].rearrange("p c (j r) -> p c j r", r=SEG),
+                votes[c0 // 2][:, c0 % 2 : c0 % 2 + c1 - c0, n0 * RUNS : n1 * RUNS],
+                soft[n0][:, c0:c1, :].rearrange("p c (j r) -> p c j r", r=SEG),
                 mybir.AxisListType.X,
                 mybir.AluOpType.add,
             )
 
-        def store(half):
-            rows = out[0, half * HALF_LIST : (half + 1) * HALF_LIST, :]
-            nc.sync.dma_start(rows.rearrange("(p c) j -> p c j", c=2), votes[half][:])
+        def store(h):
+            rows = out[0].rearrange("(p c) j -> p c j", c=BLOCKS)
+            nc.sync.dma_start(rows[:, 2 * h : 2 * h + 2, :], votes[h][:])
 
         interleave(on_scalar, 0, 1)
-        bias = held.tile([P, BLOCKS], F32, name="bias", tag="bias", align_bytes=64)
-        nc.scalar.activation(bias[:], turned[:, :, TT_ROW], ACT.Copy, scale=-SHARP)
+        part_words(1, 0, HALF_LIST)
+        part_words(1, HALF_LIST, SLOTS)
+        interleave(on_vector, 1, 1)
         quantise(0, 1)
-        parted = held.tile([P, 2, PASSES, HALF_LIST], U16, name="parted", tag="raw01", align_bytes=64)
-        part_words(0)
-        part_words(1)
-        early = place[0, 1][0]
-        spare = psum.tile([P, PASSES * HALF_LIST], F32, name="spare", tag="bank7")
-        for _ in range(WARM_PASSES):
-            nc.tensor.matmul_mx(
-                out=spare[:],
-                lhsT=q_codes[early][:, 0, :].bitcast(FP8X4),
-                lhsT_scale=q_scales[early][:, 0, :],
-                rhs=picked_words[:, 0:HALF_LIST].bitcast(FP4X4),
-                rhs_scale=scale_pool[:, 0:SLOTS],
-                start=True,
-                stop=True,
-            )
-
-        interleave(on_vector, 0, 0)
+        part_words(0, 0, SLOTS)
+        quantise(1, 1)
+        take_banks(0, 2, 0)
+        multiply(0, 0, 1, 1, True, False)
+        multiply(0, 1, 2, 1, False, False)
+        interleave(on_scalar, 0, 0)
         interleave(on_vector, 1, 0)
-        grouped[SCALAR_PAIR] = held.tile([P, 2, K_PASS], BF16, name="grouped", tag="dealt", align_bytes=64)
-        interleave(on_scalar, 2, 0)
-        interleave(on_scalar, 3, 0)
-        quantise(0, 0)
         quantise(1, 0)
-        take_banks(0, (0, 1, 2, 3))
-        multiply(0, range(BLOCKS), (1, 0))
-
-        for n in range(1, PIECES):
-            interleave(on_vector, n, 1)
-            if n + 1 < PIECES:
-                quantise(n + 1, 0)
-            quantise(n, 1)
-
-        votes[0] = held.tile(
-            [P, 2, NQ // SEG], F32, name="votes", tag="grouped%d" % place[2, 1][0], align_bytes=64
-        )
-        votes[1] = held.tile([P, 2, NQ // SEG], F32, name="votes", tag="votes1", align_bytes=64)
-
-        last = PIECES - 1
-        soften(0, BLOCKS - 1)
-        soften_and_count(0, BLOCKS - 1)
-        take_banks(1, (4, 5))
-        for c in range(BLOCKS):
-            multiply(1, (c,), (0, 1))
-        soften(1, BLOCKS)
-        take_banks(2, (0, 1, 2, 3))
-        multiply(2, range(BLOCKS), (0, 1))
-        soften(2, BLOCKS)
-        take_banks(last, (6, 7, 4, 5))
-        multiply(last, range(BLOCKS - 1), (0, 1))
-        multiply(last, (BLOCKS - 1,), (0, 1))
-        soften(last, BLOCKS - 1)
-        soften_and_count(last, BLOCKS - 1)
-        for n in range(last):
-            count(n, 0, 2)
-            count(n, 2, BLOCKS - 1 if n == 0 else BLOCKS)
-        count(last, 0, 1)
-        count(last, 1, 2)
+        quantise(0, 0)
+        multiply(0, 0, 2, 0, False, True)
+        interleave(on_vector, 2, 0)
+        interleave(on_scalar, 3, 0)
+        take_soft(0, 2, "raw20")
+        soften(0, range(BLOCKS))
+        quantise(2, 0)
+        quantise(3, 0)
+        take_banks(2, 3, 4)
+        multiply(2, 2, 3, 0, True, False)
+        interleave(on_vector, 2, 1, "grouped30")
+        count(0, 2, 0, 1)
+        quantise(2, 1)
+        multiply(2, 2, 3, 1, False, True)
+        interleave(on_vector, 3, 1)
+        count(0, 2, 1, 2)
+        take_banks(3, 4, 0)
+        multiply(3, 3, 4, 0, True, False)
+        quantise(3, 1)
+        take_soft(2, 3, "soft2")
+        soften(2, range(BLOCKS))
+        multiply(3, 3, 4, 1, False, True)
+        count(0, 2, 2, 4)
+        take_soft(3, 4, "soft3")
+        soften(3, range(BLOCKS - 1))
+        soften_and_count(3, BLOCKS - 1)
+        count(2, 3, 0, 2)
+        count(2, 3, 2, 4)
+        count(3, 4, 0, 2)
         store(0)
-        count(last, 2, 3)
+        count(3, 4, 2, 3)
         store(1)

@@ -10,6 +10,7 @@ D, T, SLOTS, NQ, SEG = 1024, 2048, 512, 512, 32
 PASSES = D // K_PASS
 BLOCKS = SLOTS // P
 PIECE = 128
+PIECES = NQ // PIECE
 RUNS = PIECE // SEG
 SHARP = 4.0
 LIVE = 96
@@ -58,21 +59,17 @@ def tile_attend_tok_votets_topk_kernel(tc, qT, k_words, k_scales, tt, offs, out)
 
         raw = {}
 
-        raw_tiles = {}
-
-        def load_queries(o, n0, n1, t0=0, t1=PACK):
-            if t0 == 0:
-                raw_tiles[n0, o] = held.tile(
-                    [P, PACK, (n1 - n0) * PIECE], F32, name="raw", tag="raw%d%d" % (n0, o), align_bytes=64
-                )
-            tile = raw_tiles[n0, o]
+        def load_queries(o, n0, n1):
+            tile = held.tile(
+                [P, PACK, (n1 - n0) * PIECE], F32, name="raw", tag="raw%d%d" % (n0, o), align_bytes=64
+            )
             rows = qT[0, o * K_PASS : (o + 1) * K_PASS, n0 * PIECE : n1 * PIECE]
-            nc.sync.dma_start(tile[:, t0:t1, :], rows.rearrange("(p j) w -> p j w", j=PACK)[:, t0:t1, :])
+            nc.sync.dma_start(tile[:], rows.rearrange("(p j) w -> p j w", j=PACK))
             for n in range(n0, n1):
                 raw[n, o] = tile[:, :, (n - n0) * PIECE : (n - n0 + 1) * PIECE]
 
         load_queries(1, 0, 2)
-        load_queries(0, 0, 2, 0, 2)
+        load_queries(0, 0, 2)
 
         picked_scales = held.tile([P, SLOTS], U8, name="picked_scales", align_bytes=64)
         nc.vector.tensor_copy(
@@ -84,7 +81,6 @@ def tile_attend_tok_votets_topk_kernel(tc, qT, k_words, k_scales, tt, offs, out)
                 key_scales[32 * quad : 32 * quad + 4].rearrange("p o n -> p (o n)").bitcast(I32),
                 picked_scales[LIVE + 8 * quad : LIVE + 8 * quad + 8, :].bitcast(I32),
             )
-        load_queries(0, 0, 2, 2, PACK)
         load_queries(0, 2, 4)
         load_queries(1, 2, 3)
         load_queries(1, 3, 4)
@@ -112,14 +108,6 @@ def tile_attend_tok_votets_topk_kernel(tc, qT, k_words, k_scales, tt, offs, out)
             )
 
         grouped, q_codes, q_scales = {}, {}, {}
-        for o in range(PASSES):
-            for half in range(2):
-                q_codes[half, o] = held.tile(
-                    [P, 2 * PIECE], U32, name="q_codes", tag="codes%d%d" % (half, o), align_bytes=64
-                )
-                q_scales[half, o] = held.tile(
-                    [P, 2 * PIECE], U8, name="q_scales", tag="q_scales%d%d" % (half, o), align_bytes=64
-                )
         on_scalar, on_vector = nc.scalar.copy, nc.vector.tensor_copy
 
         def interleave(copy, n, o, tag=None):
@@ -131,45 +119,41 @@ def tile_attend_tok_votets_topk_kernel(tc, qT, k_words, k_scales, tt, offs, out)
                 raw[n, o].rearrange("p t (c i) -> p c t i", i=4),
             )
 
-        def quantise(n, o):
-            cols = slice(n % 2 * PIECE, (n % 2 + 1) * PIECE)
+        def quantise(n, o, tag=None):
+            q_codes[n, o] = held.tile(
+                [P, PIECE], U32, name="q_codes", tag=tag or "codes%d%d" % (n, o), align_bytes=64
+            )
+            q_scales[n, o] = held.tile(
+                [P, PIECE], U8, name="q_scales", tag="q_scales%d%d" % (n, o), align_bytes=64
+            )
             nc.vector.quantize_mx(
-                out=q_codes[n // 2, o][:, cols].bitcast(FP8X4),
-                scales=q_scales[n // 2, o][:, cols],
-                in_=grouped[n, o][:],
+                out=q_codes[n, o][:].bitcast(FP8X4), scales=q_scales[n, o][:], in_=grouped[n, o][:]
             )
 
         banks, soft = {}, {}
 
-        def take_banks(n0, n1, first_bank):
+        def multiply(n, o, start):
             for c in range(BLOCKS):
-                bank = psum.tile([P, (n1 - n0) * PIECE], F32, name="acc", tag="bank%d" % (first_bank + c))
-                banks[n0, c] = bank[:]
-
-        def multiply(group, n0, n1, o, start, stop):
-            cols = slice(n0 % 2 * PIECE, n0 % 2 * PIECE + (n1 - n0) * PIECE)
-            for c in range(BLOCKS):
+                if start:
+                    number = n % 2 * BLOCKS + c
+                    banks[n, c] = psum.tile([P, PIECE], F32, name="acc", tag="bank%d" % number)
                 nc.tensor.matmul_mx(
-                    out=banks[group, c][:, (n0 - group) * PIECE : (n1 - group) * PIECE],
+                    out=banks[n, c][:],
                     lhsT=key_words[:, o, c * P : (c + 1) * P].bitcast(FP4X4),
                     lhsT_scale=key_scales[:, o, c * P : (c + 1) * P],
-                    rhs=q_codes[n0 // 2, o][:, cols].bitcast(FP8X4),
-                    rhs_scale=q_scales[n0 // 2, o][:, cols],
+                    rhs=q_codes[n, o][:].bitcast(FP8X4),
+                    rhs_scale=q_scales[n, o][:],
                     start=start,
-                    stop=stop,
+                    stop=not start,
                 )
 
-        votes = [
-            held.tile([P, 2, NQ // SEG], F32, name="votes", tag="votes%d" % h, align_bytes=64) for h in range(2)
-        ]
+        votes = {}
 
-        def take_soft(n0, n1, tag):
-            soft[n0] = held.tile([P, BLOCKS, (n1 - n0) * PIECE], F32, name="soft", tag=tag, align_bytes=64)
-
-        def soften(n0, blocks):
-            for c in blocks:
+        def soften(n, blocks):
+            soft[n] = held.tile([P, BLOCKS, PIECE], F32, name="soft", tag="soft%d" % n, align_bytes=64)
+            for c in range(blocks):
                 nc.scalar.activation(
-                    soft[n0][:, c, :], banks[n0, c], ACT.Sigmoid, bias=bias[:, c : c + 1], scale=SHARP
+                    soft[n][:, c, :], banks[n, c][:], ACT.Sigmoid, bias=bias[:, c : c + 1], scale=SHARP
                 )
 
         def soften_and_count(n, c):
@@ -183,10 +167,10 @@ def tile_attend_tok_votets_topk_kernel(tc, qT, k_words, k_scales, tt, offs, out)
                     accum_out=votes[c // 2][:, c % 2, n * RUNS + j : n * RUNS + j + 1],
                 )
 
-        def count(n0, n1, c0, c1):
+        def count(n, c0, c1):
             nc.vector.tensor_reduce(
-                votes[c0 // 2][:, c0 % 2 : c0 % 2 + c1 - c0, n0 * RUNS : n1 * RUNS],
-                soft[n0][:, c0:c1, :].rearrange("p c (j r) -> p c j r", r=SEG),
+                votes[c0 // 2][:, c0 % 2 : c0 % 2 + c1 - c0, n * RUNS : (n + 1) * RUNS],
+                soft[n][:, c0:c1, :].rearrange("p c (j r) -> p c j r", r=SEG),
                 mybir.AxisListType.X,
                 mybir.AluOpType.add,
             )
@@ -202,41 +186,40 @@ def tile_attend_tok_votets_topk_kernel(tc, qT, k_words, k_scales, tt, offs, out)
         quantise(0, 1)
         part_words(0, 0, SLOTS)
         quantise(1, 1)
-        take_banks(0, 2, 0)
-        multiply(0, 0, 1, 1, True, False)
-        multiply(0, 1, 2, 1, False, False)
-        interleave(on_scalar, 0, 0)
-        interleave(on_vector, 1, 0)
-        quantise(1, 0)
+        interleave(on_vector, 0, 0)
+        interleave(on_scalar, 1, 0)
         quantise(0, 0)
-        multiply(0, 0, 2, 0, False, True)
+        quantise(1, 0)
+        multiply(0, 1, True)
+        multiply(0, 0, False)
+        multiply(1, 1, True)
+        multiply(1, 0, False)
         interleave(on_vector, 2, 0)
-        interleave(on_scalar, 3, 0)
-        take_soft(0, 2, "raw20")
-        soften(0, range(BLOCKS))
+        interleave(on_vector, 3, 0)
         quantise(2, 0)
-        quantise(3, 0)
-        take_banks(2, 3, 4)
-        multiply(2, 2, 3, 0, True, False)
-        interleave(on_vector, 2, 1, "grouped30")
-        count(0, 2, 0, 1)
+        interleave(on_vector, 2, 1)
+        quantise(3, 0, "raw21")
         quantise(2, 1)
-        multiply(2, 2, 3, 1, False, True)
         interleave(on_vector, 3, 1)
-        count(0, 2, 1, 2)
-        take_banks(3, 4, 0)
-        multiply(3, 3, 4, 0, True, False)
+        votes[0] = held.tile([P, 2, NQ // SEG], F32, name="votes", tag="raw31", align_bytes=64)
+        votes[1] = held.tile([P, 2, NQ // SEG], F32, name="votes", tag="votes1", align_bytes=64)
+        for n in range(2):
+            soften(n, 2)
+            soften_and_count(n, 2)
+            soften_and_count(n, 3)
+        multiply(2, 0, True)
+        count(0, 0, 2)
         quantise(3, 1)
-        take_soft(2, 3, "soft2")
-        soften(2, range(BLOCKS))
-        multiply(3, 3, 4, 1, False, True)
-        count(0, 2, 2, 4)
-        take_soft(3, 4, "soft3")
-        soften(3, range(BLOCKS - 1))
+        multiply(2, 1, False)
+        soften(2, BLOCKS)
+        multiply(3, 0, True)
+        multiply(3, 1, False)
+        soften(3, BLOCKS - 1)
         soften_and_count(3, BLOCKS - 1)
-        count(2, 3, 0, 2)
-        count(2, 3, 2, 4)
-        count(3, 4, 0, 2)
+        count(1, 0, 2)
+        count(2, 0, 2)
+        count(2, 2, 4)
+        count(3, 0, 2)
         store(0)
-        count(3, 4, 2, 3)
+        count(3, 2, 3)
         store(1)

@@ -73,7 +73,7 @@ def tile_attend_tok_votets_topk_kernel(tc, qT, k_words, k_scales, tt, offs, out)
 
         picked_scales = held.tile([P, SLOTS], U8, name="picked_scales", align_bytes=64)
         nc.vector.tensor_copy(
-            picked_scales[:].rearrange("p (c q) -> p q c", c=BLOCKS), scale_pool[:].indirect(offsets[:])
+            picked_scales[:].rearrange("p (h c q) -> p h q c", h=2, c=2), scale_pool[:].indirect(offsets[:])
         )
         key_scales = held.tile([P, PASSES, SLOTS], U8, name="key_scales", align_bytes=64)
         for quad in (0, 2, 1, 3):
@@ -89,7 +89,8 @@ def tile_attend_tok_votets_topk_kernel(tc, qT, k_words, k_scales, tt, offs, out)
         nc.scalar.activation(picked_tt[:], tt_pool[:].indirect(offsets[:]), ACT.Copy)
         turned = psum.tile([P, BLOCKS, P], F32, name="turned", tag="bank7")
         for c in range(BLOCKS):
-            nc.tensor.transpose(turned[:, c, :], picked_tt[:, c:SLOTS:BLOCKS], ident[:])
+            s0 = c // 2 * HALF_LIST
+            nc.tensor.transpose(turned[:, c, :], picked_tt[:, s0 + c % 2 : s0 + HALF_LIST : 2], ident[:])
         bias = held.tile([P, BLOCKS], F32, name="bias", align_bytes=64)
         nc.scalar.activation(bias[:], turned[:, :, TT_ROW], ACT.Copy, scale=-SHARP)
 
@@ -103,8 +104,10 @@ def tile_attend_tok_votets_topk_kernel(tc, qT, k_words, k_scales, tt, offs, out)
 
         def part_words(o, s0, s1):
             nc.vector.tensor_copy(
-                key_words[:, o, :].rearrange("p (c q) -> p q c", c=BLOCKS)[:, s0 // BLOCKS : s1 // BLOCKS, :],
-                picked_words[:, s0:s1].bitcast(U16).rearrange("p (q c o) -> p o q c", c=BLOCKS, o=PASSES)[:, o],
+                key_words[:, o, s0:s1].rearrange("p (h c q) -> p h q c", c=2, q=P),
+                picked_words[:, s0:s1]
+                .bitcast(U16)
+                .rearrange("p (h q c o) -> p o h q c", q=P, c=2, o=PASSES)[:, o],
             )
 
         grouped, q_codes, q_scales = {}, {}, {}
@@ -176,8 +179,8 @@ def tile_attend_tok_votets_topk_kernel(tc, qT, k_words, k_scales, tt, offs, out)
             )
 
         def store(h):
-            rows = out[0].rearrange("(p c) j -> p c j", c=BLOCKS)
-            nc.sync.dma_start(rows[:, 2 * h : 2 * h + 2, :], votes[h][:])
+            rows = out[0, h * HALF_LIST : (h + 1) * HALF_LIST, :]
+            nc.sync.dma_start(rows.rearrange("(p c) j -> p c j", c=2), votes[h][:])
 
         interleave(on_scalar, 0, 1)
         part_words(1, 0, HALF_LIST)

@@ -201,10 +201,10 @@ def tile_attend_tok_votets_topk_kernel(tc, qT, k_words, k_scales, tt, offs, out)
         interleave(on_vector, 3, 0)
         quantise(2, 0)
         interleave(on_vector, 2, 1)
-        quantise(3, 0, "raw21")
         quantise(2, 1)
+        quantise(3, 0, "raw21")
         interleave(on_vector, 3, 1)
-        votes[0] = held.tile([P, 2, NQ // SEG], F32, name="votes", tag="raw31", align_bytes=64)
+        votes[0] = held.tile([P, 2, NQ // SEG], F32, name="votes", tag="grouped21", align_bytes=64)
         votes[1] = held.tile([P, 2, NQ // SEG], F32, name="votes", tag="votes1", align_bytes=64)
         for n in range(2):
             soften(n, 2)
@@ -222,7 +222,8 @@ def tile_attend_tok_votets_topk_kernel(tc, qT, k_words, k_scales, tt, offs, out)
         count(1, 0, 2)
         count(2, 0, 2)
         count(2, 2, 4)
-        count(3, 0, 2)
+        count(3, 0, 1)
+        count(3, 1, 2)
         store(0)
         count(3, 2, 3)
         store(1)

from contextlib import ExitStack

import concourse.mybir as mybir
from concourse.masks import make_identity

P = 128
PACK = 4
K_PASS = P * PACK
D, T, SLOTS, NQ, SEG = 1024, 2048, 512, 512, 32
PASSES = D // K_PASS
BLOCKS = SLOTS // P
PIECE = 128
PIECES = NQ // PIECE
RUNS = PIECE // SEG
SHARP = 4.0
LIVE = 96
TT_ROW = P - 1
HALF_LIST = SLOTS // 2

F32 = mybir.dt.float32
BF16 = mybir.dt.bfloat16
I32 = mybir.dt.int32
U32 = mybir.dt.uint32
U16 = mybir.dt.uint16
U8 = mybir.dt.uint8
FP8X4 = mybir.dt.float8_e4m3fn_x4
FP4X4 = mybir.dt.float4_e2m1fn_x4
ACT = mybir.ActivationFunctionType

FLOPS = 2 * SLOTS * NQ * D
BYTES = 4 * D * NQ + P * T * 4 + PASSES * 16 * T + 4 * T + 2 * P * SLOTS // 16 + 4 * SLOTS * NQ // SEG


def tile_attend_tok_votets_topk_kernel(tc, qT, k_words, k_scales, tt, offs, out):
    nc = tc.nc
    with ExitStack() as ctx:
        held = ctx.enter_context(tc.tile_pool(name="held", bufs=1))
        psum = ctx.enter_context(tc.psum_pool(name="psum", bufs=1))

        scale_pool = held.tile([P, T], U8, name="scale_pool", align_bytes=64)
        nc.sync.dma_start(
            scale_pool[LIVE:P, :].bitcast(I32), k_scales.rearrange("o f t -> f o t").bitcast(I32)
        )
        offsets = held.tile([P, SLOTS // 16], U16, name="offsets")
        nc.sync.dma_start(offsets[:], offs)
        tt_pool = held.tile([P, T], F32, name="tt_pool", align_bytes=64)
        nc.scalar.dma_start(tt_pool[TT_ROW:P, :], tt[0:1, :])
        word_pool = held.tile([P, T], U32, name="word_pool", align_bytes=64)
        nc.sync.dma_start(
            word_pool[:].bitcast(I32), k_words[0].rearrange("p t b -> p (t b)").bitcast(I32)
        )
        warm = held.tile([P, 16], F32, name="warm", align_bytes=64)
        nc.gpsimd.memset(warm[:, 0:8], 0.0)
        nc.scalar.activation(warm[:, 8:16], warm[:, 0:8], ACT.Sigmoid)
        nc.vector.memset(scale_pool[0:LIVE, :].bitcast(I32), 0)
        nc.vector.memset(tt_pool[0:TT_ROW, :].bitcast(I32), 0)
        ident = held.tile([P, P], F32, name="ident")
        make_identity(nc, ident[:])

        raw = {}

        def load_queries(o, n0, n1):
            tile = held.tile(
                [P, PACK, (n1 - n0) * PIECE], F32, name="raw", tag="raw%d%d" % (n0, o), align_bytes=64
            )
            rows = qT[0, o * K_PASS : (o + 1) * K_PASS, n0 * PIECE : n1 * PIECE]
            nc.sync.dma_start(tile[:], rows.rearrange("(p j) w -> p j w", j=PACK))
            for n in range(n0, n1):
                raw[n, o] = tile[:, :, (n - n0) * PIECE : (n - n0 + 1) * PIECE]

        load_queries(1, 0, 2)
        load_queries(0, 0, 2)

        picked_scales = held.tile([P, SLOTS], U8, name="picked_scales", align_bytes=64)
        nc.vector.tensor_copy(
            picked_scales[:].rearrange("p (h c q) -> p h q c", h=2, c=2), scale_pool[:].indirect(offsets[:])
        )
        key_scales = held.tile([P, PASSES, SLOTS], U8, name="key_scales", align_bytes=64)
        for quad in (0, 2, 1, 3):
            nc.sync.dma_start(
                key_scales[32 * quad : 32 * quad + 4].rearrange("p o n -> p (o n)").bitcast(I32),
                picked_scales[LIVE + 8 * quad : LIVE + 8 * quad + 8, :].bitcast(I32),
            )
        load_queries(0, 2, 4)
        load_queries(1, 2, 3)
        load_queries(1, 3, 4)

        picked_tt = held.tile([P, SLOTS], F32, name="picked_tt", align_bytes=64)
        nc.scalar.activation(picked_tt[:], tt_pool[:].indirect(offsets[:]), ACT.Copy)
        turned = psum.tile([P, BLOCKS, P], F32, name="turned", tag="bank7")
        for c in range(BLOCKS):
            s0 = c // 2 * HALF_LIST
            nc.tensor.transpose(turned[:, c, :], picked_tt[:, s0 + c % 2 : s0 + HALF_LIST : 2], ident[:])
        bias = held.tile([P, BLOCKS], F32, name="bias", align_bytes=64)
        nc.scalar.activation(bias[:], turned[:, :, TT_ROW], ACT.Copy, scale=-SHARP)

        picked_words = held.tile([P, SLOTS], U32, name="picked_words", align_bytes=64)
        for s0 in range(0, SLOTS, HALF_LIST):
            nc.vector.tensor_copy(
                picked_words[:, s0 : s0 + HALF_LIST],
                word_pool[:].indirect(offsets[:, s0 // 16 : (s0 + HALF_LIST) // 16]),
            )
        key_words = held.tile([P, PASSES, SLOTS], U16, name="key_words", align_bytes=64)

        def part_words(o, s0, s1):
            nc.vector.tensor_copy(
                key_words[:, o, s0:s1].rearrange("p (h c q) -> p h q c", c=2, q=P),
                picked_words[:, s0:s1]
                .bitcast(U16)
                .rearrange("p (h q c o) -> p o h q c", q=P, c=2, o=PASSES)[:, o],
            )

        grouped, q_codes, q_scales = {}, {}, {}
        on_scalar, on_vector = nc.scalar.copy, nc.vector.tensor_copy

        def interleave(copy, n, o, tag=None):
            grouped[n, o] = held.tile(
                [P, K_PASS], BF16, name="grouped", tag=tag or "grouped%d%d" % (n, o), align_bytes=64
            )
            copy(
                grouped[n, o][:].rearrange("p (c i t) -> p c t i", i=4, t=PACK),
                raw[n, o].rearrange("p t (c i) -> p c t i", i=4),
            )

        def quantise(n, o, tag=None):
            q_codes[n, o] = held.tile(
                [P, PIECE], U32, name="q_codes", tag=tag or "codes%d%d" % (n, o), align_bytes=64
            )
            q_scales[n, o] = held.tile(
                [P, PIECE], U8, name="q_scales", tag="q_scales%d%d" % (n, o), align_bytes=64
            )
            nc.vector.quantize_mx(
                out=q_codes[n, o][:].bitcast(FP8X4), scales=q_scales[n, o][:], in_=grouped[n, o][:]
            )

        banks, soft = {}, {}

        def multiply(n, o, start):
            for c in range(BLOCKS):
                if start:
                    number = n % 2 * BLOCKS + c
                    banks[n, c] = psum.tile([P, PIECE], F32, name="acc", tag="bank%d" % number)
                nc.tensor.matmul_mx(
                    out=banks[n, c][:],
                    lhsT=key_words[:, o, c * P : (c + 1) * P].bitcast(FP4X4),
                    lhsT_scale=key_scales[:, o, c * P : (c + 1) * P],
                    rhs=q_codes[n, o][:].bitcast(FP8X4),
                    rhs_scale=q_scales[n, o][:],
                    start=start,
                    stop=not start,
                )

        votes = {}

        def soften(n, blocks):
            soft[n] = held.tile([P, BLOCKS, PIECE], F32, name="soft", tag="soft%d" % n, align_bytes=64)
            for c in range(blocks):
                nc.scalar.activation(
                    soft[n][:, c, :], banks[n, c][:], ACT.Sigmoid, bias=bias[:, c : c + 1], scale=SHARP
                )

        def soften_and_count(n, c):
            for j in range(RUNS):
                nc.scalar.activation(
                    soft[n][:, c, j * SEG : (j + 1) * SEG],
                    banks[n, c][:, j * SEG : (j + 1) * SEG],
                    ACT.Sigmoid,
                    bias=bias[:, c : c + 1],
                    scale=SHARP,
                    accum_out=votes[c // 2][:, c % 2, n * RUNS + j : n * RUNS + j + 1],
                )

        def count(n, c0, c1):
            nc.vector.tensor_reduce(
                votes[c0 // 2][:, c0 % 2 : c0 % 2 + c1 - c0, n * RUNS : (n + 1) * RUNS],
                soft[n][:, c0:c1, :].rearrange("p c (j r) -> p c j r", r=SEG),
                mybir.AxisListType.X,
                mybir.AluOpType.add,
            )

        def store(h):
            rows = out[0, h * HALF_LIST : (h + 1) * HALF_LIST, :]
            nc.sync.dma_start(rows.rearrange("(p c) j -> p c j", c=2), votes[h][:])

        interleave(on_scalar, 0, 1)
        part_words(1, 0, HALF_LIST)
        part_words(1, HALF_LIST, SLOTS)
        interleave(on_vector, 1, 1)
        quantise(0, 1)
        part_words(0, 0, SLOTS)
        quantise(1, 1)
        interleave(on_vector, 0, 0)
        interleave(on_scalar, 1, 0)
        quantise(0, 0)
        quantise(1, 0)
        multiply(0, 1, True)
        multiply(0, 0, False)
        multiply(1, 1, True)
        multiply(1, 0, False)
        interleave(on_vector, 2, 0)
        interleave(on_vector, 3, 0)
        quantise(2, 0)
        interleave(on_vector, 2, 1)
        quantise(2, 1)
        quantise(3, 0, "raw21")
        interleave(on_vector, 3, 1)
        votes[0] = held.tile([P, 2, NQ // SEG], F32, name="votes", tag="grouped21", align_bytes=64)
        votes[1] = held.tile([P, 2, NQ // SEG], F32, name="votes", tag="votes1", align_bytes=64)
        for n in range(2):
            soften(n, 2)
            soften_and_count(n, 2)
            soften_and_count(n, 3)
        multiply(2, 0, True)
        count(0, 0, 2)
        quantise(3, 1)
        multiply(2, 1, False)
        soften(2, BLOCKS)
        multiply(3, 0, True)
        multiply(3, 1, False)
        soften(3, BLOCKS - 1)
        soften_and_count(3, BLOCKS - 1)
        count(1, 0, 2)
        count(2, 0, 2)
        count(2, 2, 4)
        count(3, 0, 1)
        count(3, 1, 2)
        store(0)
        count(3, 2, 3)
        store(1)
